import numpy as np
import ml_dtypes


def mxq(x, axis, fmt="e4m3"):
    dtype, down = {"e4m3": (ml_dtypes.float8_e4m3fn, 7), "e5m2": (ml_dtypes.float8_e5m2, 14)}[fmt]
    v = np.moveaxis(np.asarray(x, np.float32).astype(ml_dtypes.bfloat16).astype(np.float64), axis, -1)
    blocks = v.reshape(v.shape[:-1] + (-1, 32))
    amax = np.abs(blocks).max(-1, keepdims=True)
    byte = np.maximum(np.where(amax > 0, np.frexp(amax)[1] - 1 + 127, 0) - down, 1)
    scale = np.exp2(byte - 127.0)
    codes = (blocks / scale).astype(np.float32).astype(dtype).astype(np.float64)
    return np.moveaxis((codes * scale).reshape(v.shape), -1, axis)


WIDE = False


def mx_kscale(k):
    if not WIDE:
        return np.ones(k)
    levels = np.array([10, -10, 5, -5, 0])
    if k % 512:
        return np.exp2(np.random.permutation(np.resize(levels, k // 32))).repeat(32)
    a = np.empty((k // 512, 16))
    for p in range(k // 512):
        a[p, :8] = np.random.permutation(np.resize(levels, 8))
        for g in range(8):
            far = levels[np.abs(levels - a[p, g]) >= 10]
            a[p, g + 8] = far[np.random.randint(len(far))]
    return np.exp2(a.ravel()).repeat(32)


def f64(x):
    return np.asarray(x).astype(np.float64)


def striped(idx):
    return np.tile(idx.reshape(-1, 16).T, (8, 1)).astype(np.uint16)


def unstriped(offs):
    return offs[:16].T.reshape(-1).astype(np.int64)


def pack_weight(w):
    k, n = w.shape
    w = f64(np.asarray(w, np.float32).astype(ml_dtypes.bfloat16)).reshape(k // 32, 32, n)
    amax = np.abs(w).max(1)
    byte = np.clip(np.where(amax > 0, np.frexp(amax)[1] - 1 + 127 - 7, 1), 1, 254)
    scaled = (w * np.exp2(127.0 - byte)[:, None, :]).reshape(k, n).astype(np.float32)
    words = np.ascontiguousarray(scaled.reshape(k // 512, 128, 4, n).transpose(0, 1, 3, 2)).astype(ml_dtypes.float8_e4m3fn).view(np.uint8)
    return words, np.ascontiguousarray(byte.astype(np.uint8).reshape(k // 512, 16, n))


def unpack_weight(words, scales):
    g, p, n, _ = words.shape
    vals = np.ascontiguousarray(words).view(ml_dtypes.float8_e4m3fn).astype(np.float64) * np.repeat(np.exp2(scales.astype(np.float64) - 127.0), 8, axis=1)[..., None]
    return vals.transpose(0, 1, 3, 2).reshape(g * 512, n)

def planes(y):
    n, m = y.shape
    v = y.astype(np.float32).astype(ml_dtypes.bfloat16).astype(np.float64).reshape(n // 32, 32, m)
    top = np.abs(v).max(1)
    byte = np.clip(np.where(top > 0, np.frexp(top)[1] - 1 + 127 - 7, 1), 1, 254)
    codes = (v * np.exp2(127.0 - byte)[:, None, :]).reshape(n, m).astype(np.float32).astype(ml_dtypes.float8_e4m3fn).view(np.uint8)
    words = codes.reshape(n // 512, 128, 4, m).transpose(0, 1, 3, 2)
    return np.ascontiguousarray(words), np.ascontiguousarray(byte.astype(np.uint8).reshape(n // 512, 16, m))


K, T, N, U = 512, 512, 512, 1024


def setup_inputs():
    n = np.random.standard_normal
    s = mx_kscale(K)[:, None]
    packed_xT = pack_weight(n((K, T)) * s)
    return {
        "x_words": packed_xT[0],
        "x_scales": packed_xT[1],
        "mem": n((N, U)).astype(np.float32),
        "w1": (n((K, N)) / np.sqrt(K) / s).astype(np.float32),
        "slot": striped(np.random.permutation(U)[:T]),
    }


def reference(x_words, x_scales, mem, w1, slot):
    xq = unpack_weight(x_words, x_scales)
    y = mxq(f64(w1), 0, "e4m3").T @ xq
    out = f64(mem).copy()
    out[:, unstriped(slot)] = np.minimum(f64(mem)[:, unstriped(slot)], y)
    return (out,) + planes(out)

@@ -1,0 +1,117 @@
+from contextlib import ExitStack
+
+import concourse.mybir as mybir
+
+K, T, N, U = 512, 512, 512, 1024
+FLOPS = 2 * K * T * N
+
+F32 = mybir.dt.float32
+BF16 = mybir.dt.bfloat16
+I32 = mybir.dt.int32
+U32 = mybir.dt.uint32
+U16 = mybir.dt.uint16
+U8 = mybir.dt.uint8
+FP8X4 = mybir.dt.float8_e4m3fn_x4
+MIN = mybir.AluOpType.min
+
+P = 128
+PACK = 4
+W_CHUNKS = 2
+OUT_CHUNKS = 4
+VECTOR_CHUNKS = 2
+
+
+def tile_picked_widxput_min_lo_kernel(tc, x_words, x_scales, mem, w1, slot, out_0, out_1, out_2):
+    nc = tc.nc
+    with ExitStack() as ctx:
+        keep = ctx.enter_context(tc.tile_pool(name="keep", bufs=1))
+        psum = ctx.enter_context(tc.psum_pool(name="psum", bufs=1))
+
+        offsets = keep.tile([P, T // 16], U16, name="offsets")
+        nc.sync.dma_start(offsets[:], slot)
+
+        x_scale = keep.tile([P, T], U8, name="x_scale", align_bytes=64)
+        nc.vector.memset(x_scale[:].bitcast(I32), 0)
+        x_scale_rows = x_scales[0].bitcast(I32)
+        for q in range(4):
+            nc.scalar.dma_start(x_scale[32 * q : 32 * q + 4, :].bitcast(I32), x_scale_rows[4 * q : 4 * q + 4, :])
+
+        w_rows = w1.rearrange("(p j) c -> p j c", j=PACK)
+        wc = N // W_CHUNKS
+        w_raw = []
+        for h in range(W_CHUNKS):
+            raw = keep.tile([P, PACK, wc], F32, name=f"w_raw{h}")
+            nc.sync.dma_start(raw[:], w_rows[:, :, h * wc : (h + 1) * wc])
+            w_raw.append(raw)
+
+        mem_rows = mem.rearrange("(p t) u -> p t u", t=PACK)
+        out_rows = out_0.rearrange("(p t) u -> p t u", t=PACK)
+        store = [keep.tile([P, U], F32, name=f"store{t}") for t in range(PACK)]
+        nc.sync.dma_start(store[0][:], mem_rows[:, 0, :])
+        x_codes = keep.tile([P, T], U32, name="x_codes", align_bytes=64)
+        nc.sync.dma_start(x_codes[:].bitcast(I32), x_words[0].rearrange("p c r -> p (c r)").bitcast(I32))
+        for t in range(1, PACK):
+            nc.sync.dma_start(store[t][:], mem_rows[:, t, :])
+
+        w_grouped = keep.tile([P, PACK, P, PACK], BF16, name="w_grouped", align_bytes=64)
+        mc = wc // PACK
+        for h in range(W_CHUNKS):
+            nc.vector.tensor_copy(
+                w_grouped[:, :, h * mc : (h + 1) * mc, :].rearrange("p t m j -> p m t j"),
+                w_raw[h][:].rearrange("p j (m t) -> p m t j", t=PACK),
+            )
+        y = []
+        for t in range(PACK):
+            w_codes = keep.tile([P, P], U32, name=f"w_codes{t}", align_bytes=64)
+            w_scale = keep.tile([P, P], U8, name=f"w_scale{t}", align_bytes=64)
+            nc.vector.quantize_mx(
+                out=w_codes[:].bitcast(FP8X4), scales=w_scale[:], in_=w_grouped[:, t, :, :].rearrange("p m j -> p (m j)")
+            )
+            bank = psum.tile([P, T], F32, name=f"y{t}")
+            nc.tensor.matmul_mx(
+                out=bank[:],
+                lhsT=w_codes[:].bitcast(FP8X4),
+                lhsT_scale=w_scale[:],
+                rhs=x_codes[:].bitcast(FP8X4),
+                rhs_scale=x_scale[:],
+                start=True,
+                stop=True,
+            )
+            y.append(bank)
+
+        oc = U // OUT_CHUNKS
+        grouped = [keep.tile([P, oc, PACK], BF16, name=f"grouped{c}", align_bytes=64) for c in range(OUT_CHUNKS)]
+        picked = [keep.tile([P, T], F32, name=f"picked{t}") for t in range(PACK)]
+
+        def gather(t):
+            nc.vector.tensor_copy(picked[t][:], store[t][:].indirect(offsets[:]))
+
+        gather(0)
+        for t in range(PACK):
+            nc.vector.tensor_tensor(picked[t][:], y[t][:], picked[t][:], MIN)
+            if t + 1 < PACK:
+                gather(t + 1)
+            nc.vector.tensor_copy(store[t][:].indirect(offsets[:]), picked[t][:])
+            nc.sync.dma_start(out_rows[:, t, :], store[t][:])
+            for c in range(OUT_CHUNKS):
+                src = store[t][:, c * oc : (c + 1) * oc]
+                if t == PACK - 1 and c < VECTOR_CHUNKS:
+                    nc.vector.tensor_copy(grouped[c][:, :, t], src)
+                elif t == PACK - 2 and c < VECTOR_CHUNKS:
+                    nc.scalar.copy(grouped[c][:, :, t : t + 2], src.unsqueeze(2).to_broadcast([P, oc, 2]))
+                else:
+                    nc.scalar.copy(grouped[c][:, :, t], src)
+
+        words = out_1[0].rearrange("p c r -> p (c r)").bitcast(I32)
+        o_scale = keep.tile([P, U], U8, name="o_scale", align_bytes=64)
+        for c in range(OUT_CHUNKS):
+            o_codes = keep.tile([P, oc], U32, name=f"o_codes{c}", align_bytes=64)
+            nc.vector.quantize_mx(
+                out=o_codes[:].bitcast(FP8X4),
+                scales=o_scale[:, c * oc : (c + 1) * oc],
+                in_=grouped[c][:].rearrange("p c t -> p (c t)"),
+            )
+            nc.sync.dma_start(words[:, c * oc : (c + 1) * oc], o_codes[:].bitcast(I32))
+        scale_rows = out_2[0].bitcast(I32)
+        for q in range(4):
+            nc.scalar.dma_start(scale_rows[4 * q : 4 * q + 4, :], o_scale[32 * q : 32 * q + 4, :].bitcast(I32))

@@ -16,9 +16,10 @@ MIN = mybir.AluOpType.min
 
 P = 128
 PACK = 4
-W_CHUNKS = 2
-OUT_CHUNKS = 4
+W_VECTOR_M = 96
+CHUNKS = (256, 256, 256, 128, 128)
 VECTOR_CHUNKS = 2
+STORE_GROUPS = ((0, 1), (2,), (3, 4))
 
 
 def tile_picked_widxput_min_lo_kernel(tc, x_words, x_scales, mem, w1, slot, out_0, out_1, out_2):
@@ -27,51 +28,49 @@ def tile_picked_widxput_min_lo_kernel(tc, x_words, x_scales, mem, w1, slot, out_
         keep = ctx.enter_context(tc.tile_pool(name="keep", bufs=1))
         psum = ctx.enter_context(tc.psum_pool(name="psum", bufs=1))
 
-        offsets = keep.tile([P, T // 16], U16, name="offsets")
-        nc.sync.dma_start(offsets[:], slot)
-
         x_scale = keep.tile([P, T], U8, name="x_scale", align_bytes=64)
-        nc.vector.memset(x_scale[:].bitcast(I32), 0)
         x_scale_rows = x_scales[0].bitcast(I32)
         for q in range(4):
             nc.scalar.dma_start(x_scale[32 * q : 32 * q + 4, :].bitcast(I32), x_scale_rows[4 * q : 4 * q + 4, :])
 
         w_rows = w1.rearrange("(p j) c -> p j c", j=PACK)
-        wc = N // W_CHUNKS
-        w_raw = []
-        for h in range(W_CHUNKS):
-            raw = keep.tile([P, PACK, wc], F32, name=f"w_raw{h}")
-            nc.sync.dma_start(raw[:], w_rows[:, :, h * wc : (h + 1) * wc])
-            w_raw.append(raw)
-
         mem_rows = mem.rearrange("(p t) u -> p t u", t=PACK)
         out_rows = out_0.rearrange("(p t) u -> p t u", t=PACK)
+        w_raw = [keep.tile([P, 2, N], F32, name=f"w_raw{h}") for h in range(2)]
         store = [keep.tile([P, U], F32, name=f"store{t}") for t in range(PACK)]
-        nc.sync.dma_start(store[0][:], mem_rows[:, 0, :])
+        offsets = keep.tile([P, T // 16], U16, name="offsets")
         x_codes = keep.tile([P, T], U32, name="x_codes", align_bytes=64)
+        nc.sync.dma_start(w_raw[0][:], w_rows[:, 0:2, :])
+        nc.sync.dma_start(w_raw[1][:], w_rows[:, 2:4, :])
+        nc.sync.dma_start(offsets[:], slot)
+        nc.sync.dma_start(store[0][:], mem_rows[:, 0, :])
+        nc.sync.dma_start(store[1][:], mem_rows[:, 1, :])
         nc.sync.dma_start(x_codes[:].bitcast(I32), x_words[0].rearrange("p c r -> p (c r)").bitcast(I32))
-        for t in range(1, PACK):
-            nc.sync.dma_start(store[t][:], mem_rows[:, t, :])
+        nc.sync.dma_start(store[2][:], mem_rows[:, 2, :])
+        nc.sync.dma_start(store[3][:], mem_rows[:, 3, :])
 
         w_grouped = keep.tile([P, PACK, P, PACK], BF16, name="w_grouped", align_bytes=64)
-        mc = wc // PACK
-        for h in range(W_CHUNKS):
-            nc.vector.tensor_copy(
-                w_grouped[:, :, h * mc : (h + 1) * mc, :].rearrange("p t m j -> p m t j"),
-                w_raw[h][:].rearrange("p j (m t) -> p m t j", t=PACK),
-            )
+
+        def w_views(h, m0, m1):
+            dst = w_grouped[:, :, m0:m1, 2 * h : 2 * h + 2].rearrange("p t m j -> p m t j")
+            src = w_raw[h][:, :, PACK * m0 : PACK * m1].rearrange("p j (m t) -> p m t j", t=PACK)
+            return dst, src
+
+        nc.vector.tensor_copy(*w_views(0, 0, P))
+        nc.vector.tensor_copy(*w_views(1, 0, W_VECTOR_M))
+        nc.scalar.copy(*w_views(1, W_VECTOR_M, P))
+        w_codes = keep.tile([P, N], U32, name="w_codes", align_bytes=64)
+        w_scale = keep.tile([P, N], U8, name="w_scale", align_bytes=64)
+        nc.vector.quantize_mx(
+            out=w_codes[:].bitcast(FP8X4), scales=w_scale[:], in_=w_grouped[:].rearrange("p t m j -> p (t m j)")
+        )
         y = []
         for t in range(PACK):
-            w_codes = keep.tile([P, P], U32, name=f"w_codes{t}", align_bytes=64)
-            w_scale = keep.tile([P, P], U8, name=f"w_scale{t}", align_bytes=64)
-            nc.vector.quantize_mx(
-                out=w_codes[:].bitcast(FP8X4), scales=w_scale[:], in_=w_grouped[:, t, :, :].rearrange("p m j -> p (m j)")
-            )
             bank = psum.tile([P, T], F32, name=f"y{t}")
             nc.tensor.matmul_mx(
                 out=bank[:],
-                lhsT=w_codes[:].bitcast(FP8X4),
-                lhsT_scale=w_scale[:],
+                lhsT=w_codes[:, t * P : (t + 1) * P].bitcast(FP8X4),
+                lhsT_scale=w_scale[:, t * P : (t + 1) * P],
                 rhs=x_codes[:].bitcast(FP8X4),
                 rhs_scale=x_scale[:],
                 start=True,
@@ -79,39 +78,55 @@ def tile_picked_widxput_min_lo_kernel(tc, x_words, x_scales, mem, w1, slot, out_
             )
             y.append(bank)
 
-        oc = U // OUT_CHUNKS
-        grouped = [keep.tile([P, oc, PACK], BF16, name=f"grouped{c}", align_bytes=64) for c in range(OUT_CHUNKS)]
+        starts = [sum(CHUNKS[:c]) for c in range(len(CHUNKS))]
+        grouped = [keep.tile([P, n, PACK], BF16, name=f"grouped{c}", align_bytes=64) for c, n in enumerate(CHUNKS)]
         picked = [keep.tile([P, T], F32, name=f"picked{t}") for t in range(PACK)]
 
         def gather(t):
             nc.vector.tensor_copy(picked[t][:], store[t][:].indirect(offsets[:]))
 
-        gather(0)
-        for t in range(PACK):
+        def smaller(t):
             nc.vector.tensor_tensor(picked[t][:], y[t][:], picked[t][:], MIN)
-            if t + 1 < PACK:
-                gather(t + 1)
+
+        def scatter(t):
             nc.vector.tensor_copy(store[t][:].indirect(offsets[:]), picked[t][:])
             nc.sync.dma_start(out_rows[:, t, :], store[t][:])
-            for c in range(OUT_CHUNKS):
-                src = store[t][:, c * oc : (c + 1) * oc]
+            for c, n in enumerate(CHUNKS):
+                src = store[t][:, starts[c] : starts[c] + n]
                 if t == PACK - 1 and c < VECTOR_CHUNKS:
                     nc.vector.tensor_copy(grouped[c][:, :, t], src)
                 elif t == PACK - 2 and c < VECTOR_CHUNKS:
-                    nc.scalar.copy(grouped[c][:, :, t : t + 2], src.unsqueeze(2).to_broadcast([P, oc, 2]))
+                    nc.scalar.copy(grouped[c][:, :, t : t + 2], src.unsqueeze(2).to_broadcast([P, n, 2]))
                 else:
                     nc.scalar.copy(grouped[c][:, :, t], src)
 
+        gather(0)
+        gather(1)
+        smaller(0)
+        smaller(1)
+        scatter(0)
+        gather(2)
+        scatter(1)
+        smaller(2)
+        gather(3)
+        scatter(2)
+        smaller(3)
+        scatter(3)
+
         words = out_1[0].rearrange("p c r -> p (c r)").bitcast(I32)
         o_scale = keep.tile([P, U], U8, name="o_scale", align_bytes=64)
-        for c in range(OUT_CHUNKS):
-            o_codes = keep.tile([P, oc], U32, name=f"o_codes{c}", align_bytes=64)
-            nc.vector.quantize_mx(
-                out=o_codes[:].bitcast(FP8X4),
-                scales=o_scale[:, c * oc : (c + 1) * oc],
-                in_=grouped[c][:].rearrange("p c t -> p (c t)"),
-            )
-            nc.sync.dma_start(words[:, c * oc : (c + 1) * oc], o_codes[:].bitcast(I32))
+        for g, group in enumerate(STORE_GROUPS):
+            first = starts[group[0]]
+            width = sum(CHUNKS[c] for c in group)
+            o_codes = keep.tile([P, width], U32, name=f"o_codes{g}", align_bytes=64)
+            for c in group:
+                nc.vector.quantize_mx(
+                    out=o_codes[:, starts[c] - first : starts[c] - first + CHUNKS[c]].bitcast(FP8X4),
+                    scales=o_scale[:, starts[c] : starts[c] + CHUNKS[c]],
+                    in_=grouped[c][:].rearrange("p c t -> p (c t)"),
+                )
+            nc.sync.dma_start(words[:, first : first + width], o_codes[:].bitcast(I32))
         scale_rows = out_2[0].bitcast(I32)
         for q in range(4):
-            nc.scalar.dma_start(scale_rows[4 * q : 4 * q + 4, :], o_scale[32 * q : 32 * q + 4, :].bitcast(I32))
+            queue = nc.scalar if q < 2 else nc.sync
+            queue.dma_start(scale_rows[4 * q : 4 * q + 4, :], o_scale[32 * q : 32 * q + 4, :].bitcast(I32))

@@ -16,7 +16,6 @@ MIN = mybir.AluOpType.min
 
 P = 128
 PACK = 4
-W_VECTOR_M = 96
 CHUNKS = (256, 256, 256, 128, 128)
 VECTOR_CHUNKS = 2
 STORE_GROUPS = ((0, 1), (2,), (3, 4))
@@ -49,34 +48,32 @@ def tile_picked_widxput_min_lo_kernel(tc, x_words, x_scales, mem, w1, slot, out_
         nc.sync.dma_start(store[2][:], mem_rows[:, 2, :])
         nc.sync.dma_start(store[3][:], mem_rows[:, 3, :])
 
-        w_grouped = keep.tile([P, PACK, P, PACK], BF16, name="w_grouped", align_bytes=64)
-
-        def w_views(h, m0, m1):
-            dst = w_grouped[:, :, m0:m1, 2 * h : 2 * h + 2].rearrange("p t m j -> p m t j")
-            src = w_raw[h][:, :, PACK * m0 : PACK * m1].rearrange("p j (m t) -> p m t j", t=PACK)
-            return dst, src
-
-        nc.vector.tensor_copy(*w_views(0, 0, P))
-        nc.vector.tensor_copy(*w_views(1, 0, W_VECTOR_M))
-        nc.scalar.copy(*w_views(1, W_VECTOR_M, P))
-        w_codes = keep.tile([P, N], U32, name="w_codes", align_bytes=64)
-        w_scale = keep.tile([P, N], U8, name="w_scale", align_bytes=64)
-        nc.vector.quantize_mx(
-            out=w_codes[:].bitcast(FP8X4), scales=w_scale[:], in_=w_grouped[:].rearrange("p t m j -> p (t m j)")
-        )
+        w_grouped = [keep.tile([P, 2, P, PACK], BF16, name=f"w_grouped{a}", align_bytes=64) for a in range(2)]
+        for h in range(2):
+            for a in range(2):
+                nc.vector.tensor_copy(
+                    w_grouped[a][:, :, :, 2 * h : 2 * h + 2].rearrange("p t (m i) j -> p m t i j", i=2),
+                    w_raw[h][:].rearrange("p j (m i t) -> p m t i j", i=2, t=PACK)[:, :, 2 * a : 2 * a + 2, :, :],
+                )
         y = []
-        for t in range(PACK):
-            bank = psum.tile([P, T], F32, name=f"y{t}")
-            nc.tensor.matmul_mx(
-                out=bank[:],
-                lhsT=w_codes[:, t * P : (t + 1) * P].bitcast(FP8X4),
-                lhsT_scale=w_scale[:, t * P : (t + 1) * P],
-                rhs=x_codes[:].bitcast(FP8X4),
-                rhs_scale=x_scale[:],
-                start=True,
-                stop=True,
+        for a in range(2):
+            w_codes = keep.tile([P, 2 * P], U32, name=f"w_codes{a}", align_bytes=64)
+            w_scale = keep.tile([P, 2 * P], U8, name=f"w_scale{a}", align_bytes=64)
+            nc.vector.quantize_mx(
+                out=w_codes[:].bitcast(FP8X4), scales=w_scale[:], in_=w_grouped[a][:].rearrange("p t m j -> p (t m j)")
             )
-            y.append(bank)
+            for e in range(2):
+                bank = psum.tile([P, T], F32, name=f"y{2 * a + e}")
+                nc.tensor.matmul_mx(
+                    out=bank[:],
+                    lhsT=w_codes[:, e * P : (e + 1) * P].bitcast(FP8X4),
+                    lhsT_scale=w_scale[:, e * P : (e + 1) * P],
+                    rhs=x_codes[:].bitcast(FP8X4),
+                    rhs_scale=x_scale[:],
+                    start=True,
+                    stop=True,
+                )
+                y.append(bank)
 
         starts = [sum(CHUNKS[:c]) for c in range(len(CHUNKS))]
         grouped = [keep.tile([P, n, PACK], BF16, name=f"grouped{c}", align_bytes=64) for c, n in enumerate(CHUNKS)]

@@ -18,7 +18,7 @@ P = 128
 PACK = 4
 CHUNKS = (256, 256, 256, 128, 128)
 VECTOR_CHUNKS = 2
-STORE_GROUPS = ((0, 1), (2,), (3, 4))
+STORE_GROUPS = ((0,), (1,), (2,), (3, 4))
 
 
 def tile_picked_widxput_min_lo_kernel(tc, x_words, x_scales, mem, w1, slot, out_0, out_1, out_2):
@@ -104,10 +104,10 @@ def tile_picked_widxput_min_lo_kernel(tc, x_words, x_scales, mem, w1, slot, out_
         scatter(0)
         gather(2)
         scatter(1)
-        smaller(2)
         gather(3)
-        scatter(2)
+        smaller(2)
         smaller(3)
+        scatter(2)
         scatter(3)
 
         words = out_1[0].rearrange("p c r -> p (c r)").bitcast(I32)

@@ -16,6 +16,7 @@ MIN = mybir.AluOpType.min
 
 P = 128
 PACK = 4
+HALF = 64
 CHUNKS = (256, 256, 256, 128, 128)
 VECTOR_CHUNKS = 2
 STORE_GROUPS = ((0,), (1,), (2,), (3, 4))
@@ -33,82 +34,123 @@ def tile_picked_widxput_min_lo_kernel(tc, x_words, x_scales, mem, w1, slot, out_
             nc.scalar.dma_start(x_scale[32 * q : 32 * q + 4, :].bitcast(I32), x_scale_rows[4 * q : 4 * q + 4, :])
 
         w_rows = w1.rearrange("(p j) c -> p j c", j=PACK)
+        mem_even = mem.rearrange("(a p e) u -> a p e u", a=2, e=2)
         mem_rows = mem.rearrange("(p t) u -> p t u", t=PACK)
+        out_even = out_0.rearrange("(a p e) u -> a p e u", a=2, e=2)
         out_rows = out_0.rearrange("(p t) u -> p t u", t=PACK)
-        w_raw = [keep.tile([P, 2, N], F32, name=f"w_raw{h}") for h in range(2)]
-        store = [keep.tile([P, U], F32, name=f"store{t}") for t in range(PACK)]
+        mem_of = [mem_even[0, :, 0, :], mem_even[1, :, 0, :], mem_rows[:, 1, :], mem_rows[:, 3, :]]
+        out_of = [out_even[0, :, 0, :], out_even[1, :, 0, :], out_rows[:, 1, :], out_rows[:, 3, :]]
+        w_raw = [keep.tile([P, PACK, N // 2], F32, name=f"w_raw{a}") for a in range(2)]
+        store = [keep.tile([P, U], F32, name=f"store{s}") for s in range(4)]
         offsets = keep.tile([P, T // 16], U16, name="offsets")
         x_codes = keep.tile([P, T], U32, name="x_codes", align_bytes=64)
-        nc.sync.dma_start(w_raw[0][:], w_rows[:, 0:2, :])
-        nc.sync.dma_start(w_raw[1][:], w_rows[:, 2:4, :])
+        nc.sync.dma_start(w_raw[0][:], w_rows[:, :, 0 : N // 2])
         nc.sync.dma_start(offsets[:], slot)
-        nc.sync.dma_start(store[0][:], mem_rows[:, 0, :])
-        nc.sync.dma_start(store[1][:], mem_rows[:, 1, :])
+        nc.sync.dma_start(store[0][:], mem_of[0])
         nc.sync.dma_start(x_codes[:].bitcast(I32), x_words[0].rearrange("p c r -> p (c r)").bitcast(I32))
-        nc.sync.dma_start(store[2][:], mem_rows[:, 2, :])
-        nc.sync.dma_start(store[3][:], mem_rows[:, 3, :])
+        nc.sync.dma_start(store[1][:], mem_of[1])
+        nc.sync.dma_start(w_raw[1][:], w_rows[:, :, N // 2 : N])
+        nc.sync.dma_start(store[2][:], mem_of[2])
+        nc.sync.dma_start(store[3][:], mem_of[3])
 
-        w_grouped = [keep.tile([P, 2, P, PACK], BF16, name=f"w_grouped{a}", align_bytes=64) for a in range(2)]
-        for h in range(2):
-            for a in range(2):
-                nc.vector.tensor_copy(
-                    w_grouped[a][:, :, :, 2 * h : 2 * h + 2].rearrange("p t (m i) j -> p m t i j", i=2),
-                    w_raw[h][:].rearrange("p j (m i t) -> p m t i j", i=2, t=PACK)[:, :, 2 * a : 2 * a + 2, :, :],
-                )
-        y = []
-        for a in range(2):
-            w_codes = keep.tile([P, 2 * P], U32, name=f"w_codes{a}", align_bytes=64)
-            w_scale = keep.tile([P, 2 * P], U8, name=f"w_scale{a}", align_bytes=64)
-            nc.vector.quantize_mx(
-                out=w_codes[:].bitcast(FP8X4), scales=w_scale[:], in_=w_grouped[a][:].rearrange("p t m j -> p (t m j)")
+        w_even = [keep.tile([P, P, PACK], BF16, name=f"w_even{a}", align_bytes=64) for a in range(2)]
+        w_odd = keep.tile([P, 2, P, PACK], BF16, name="w_odd", align_bytes=64)
+
+        def round_even(engine_copy, a):
+            engine_copy(w_even[a][:], w_raw[a][:].rearrange("p j (m e) -> p m e j", e=2)[:, :, 0, :])
+
+        def round_odd(a):
+            nc.scalar.copy(
+                w_odd[:, :, a * HALF : (a + 1) * HALF, :].rearrange("p h l j -> p l h j"),
+                w_raw[a][:].rearrange("p j (l h e) -> p l h e j", h=2, e=2)[:, :, :, 1, :],
             )
-            for e in range(2):
-                bank = psum.tile([P, T], F32, name=f"y{2 * a + e}")
-                nc.tensor.matmul_mx(
-                    out=bank[:],
-                    lhsT=w_codes[:, e * P : (e + 1) * P].bitcast(FP8X4),
-                    lhsT_scale=w_scale[:, e * P : (e + 1) * P],
-                    rhs=x_codes[:].bitcast(FP8X4),
-                    rhs_scale=x_scale[:],
-                    start=True,
-                    stop=True,
-                )
-                y.append(bank)
+
+        def quantise(grouped_w, width, name):
+            codes = keep.tile([P, width], U32, name=name + "_codes", align_bytes=64)
+            scale = keep.tile([P, width], U8, name=name + "_scale", align_bytes=64)
+            nc.vector.quantize_mx(out=codes[:].bitcast(FP8X4), scales=scale[:], in_=grouped_w)
+            return codes, scale
+
+        def project(codes, scale, e, name, first=0, width=T):
+            bank = psum.tile([P, width], F32, name=name)
+            nc.tensor.matmul_mx(
+                out=bank[:],
+                lhsT=codes[:, e * P : (e + 1) * P].bitcast(FP8X4),
+                lhsT_scale=scale[:, e * P : (e + 1) * P],
+                rhs=x_codes[:, first : first + width].bitcast(FP8X4),
+                rhs_scale=x_scale[:, first : first + width],
+                start=True,
+                stop=True,
+            )
+            return bank
 
         starts = [sum(CHUNKS[:c]) for c in range(len(CHUNKS))]
         grouped = [keep.tile([P, n, PACK], BF16, name=f"grouped{c}", align_bytes=64) for c, n in enumerate(CHUNKS)]
-        picked = [keep.tile([P, T], F32, name=f"picked{t}") for t in range(PACK)]
+        picked = {s: keep.tile([P, T], F32, name=f"picked{s}") for s in range(1, 4)}
+        moved = [keep.tile([P, 2, U // 2], F32, name=f"moved{g}") for g in range(2)]
 
-        def gather(t):
-            nc.vector.tensor_copy(picked[t][:], store[t][:].indirect(offsets[:]))
+        def move(a):
+            for g in range(2):
+                for h in range(2):
+                    nc.sync.dma_start(
+                        moved[g][a * HALF : (a + 1) * HALF, h, :], store[a][h:P:2, g * (U // 2) : (g + 1) * (U // 2)]
+                    )
+            nc.sync.dma_start(out_of[a], store[a][:])
 
-        def smaller(t):
-            nc.vector.tensor_tensor(picked[t][:], y[t][:], picked[t][:], MIN)
+        def gather(s):
+            nc.vector.tensor_copy(picked[s][:], store[s][:].indirect(offsets[:]))
 
-        def scatter(t):
-            nc.vector.tensor_copy(store[t][:].indirect(offsets[:]), picked[t][:])
-            nc.sync.dma_start(out_rows[:, t, :], store[t][:])
-            for c, n in enumerate(CHUNKS):
-                src = store[t][:, starts[c] : starts[c] + n]
-                if t == PACK - 1 and c < VECTOR_CHUNKS:
-                    nc.vector.tensor_copy(grouped[c][:, :, t], src)
-                elif t == PACK - 2 and c < VECTOR_CHUNKS:
-                    nc.scalar.copy(grouped[c][:, :, t : t + 2], src.unsqueeze(2).to_broadcast([P, n, 2]))
-                else:
-                    nc.scalar.copy(grouped[c][:, :, t], src)
+        def smaller(s, y):
+            nc.vector.tensor_tensor(picked[s][:], y[:], picked[s][:], MIN)
 
-        gather(0)
+        def scatter(s):
+            nc.vector.tensor_copy(store[s][:].indirect(offsets[:]), picked[s][:])
+
+        round_even(nc.vector.tensor_copy, 0)
+        codes, scale = quantise(w_even[0][:].rearrange("p m j -> p (m j)"), P, "w_a")
+        y_a = [project(codes, scale, 0, f"y_a{i}", i * (T // 2), T // 2) for i in range(2)]
+        round_even(nc.scalar.copy, 1)
+        round_odd(0)
+        round_odd(1)
+
+        first_picked = [keep.tile([P, T // 2], F32, name=f"first_picked{i}") for i in range(2)]
+        half_list = [offsets[:, i * (T // 32) : (i + 1) * (T // 32)] for i in range(2)]
+        for i in range(2):
+            nc.vector.tensor_copy(first_picked[i][:], store[0][:].indirect(half_list[i]))
+        for i in range(2):
+            nc.vector.tensor_tensor(first_picked[i][:], y_a[i][:], first_picked[i][:], MIN)
+        nc.vector.tensor_copy(store[0][:].indirect(half_list[0]), first_picked[0][:])
         gather(1)
-        smaller(0)
-        smaller(1)
-        scatter(0)
+        nc.vector.tensor_copy(store[0][:].indirect(half_list[1]), first_picked[1][:])
+        move(0)
+        codes, scale = quantise(w_even[1][:].rearrange("p m j -> p (m j)"), P, "w_b")
+        y_b = project(codes, scale, 0, "y_b")
         gather(2)
+        smaller(1, y_b)
+        codes, scale = quantise(w_odd[:].rearrange("p h l j -> p (h l j)"), 2 * P, "w_odd")
+        y_odd = [project(codes, scale, h, f"y_odd{h}") for h in range(2)]
         scatter(1)
+        move(1)
+        for c, n in enumerate(CHUNKS):
+            g, first = divmod(starts[c], U // 2)
+            q, first = divmod(first, U // 4)
+            quarters = moved[g][:].rearrange("p h (q c) -> p c (h q)", q=2)
+            nc.scalar.copy(grouped[c][:, :, 0:3], quarters[:, first : first + n, q : q + 3])
+
         gather(3)
-        smaller(2)
-        smaller(3)
-        scatter(2)
-        scatter(3)
+        smaller(2, y_odd[0])
+        smaller(3, y_odd[1])
+        for h in range(2):
+            scatter(2 + h)
+            nc.sync.dma_start(out_of[2 + h], store[2 + h][:])
+            for c, n in enumerate(CHUNKS):
+                src = store[2 + h][:, starts[c] : starts[c] + n]
+                if h == 0:
+                    nc.scalar.copy(grouped[c][:, :, 1:PACK:2], src.unsqueeze(2).to_broadcast([P, n, 2]))
+                elif c < VECTOR_CHUNKS:
+                    nc.vector.tensor_copy(grouped[c][:, :, 3], src)
+                else:
+                    nc.scalar.copy(grouped[c][:, :, 3], src)
 
         words = out_1[0].rearrange("p c r -> p (c r)").bitcast(I32)
         o_scale = keep.tile([P, U], U8, name="o_scale", align_bytes=64)

@@ -19,13 +19,17 @@ PACK = 4
 HALF = 64
 CHUNKS = (256, 256, 256, 128, 128)
 VECTOR_CHUNKS = 2
-STORE_GROUPS = ((0,), (1,), (2,), (3, 4))
+MOVE_WIDTHS = (256, 256, 512)
+SEAM = 16
+PICKED_AT = {1: 0, 2: 0, 3: 2048}
+STORE_GROUPS = ((0,), (1, 2), (3, 4))
 
 
 def tile_picked_widxput_min_lo_kernel(tc, x_words, x_scales, mem, w1, slot, out_0, out_1, out_2):
     nc = tc.nc
     with ExitStack() as ctx:
         keep = ctx.enter_context(tc.tile_pool(name="keep", bufs=1))
+        shared = ctx.enter_context(tc.tile_pool(name="shared", bufs=1))
         psum = ctx.enter_context(tc.psum_pool(name="psum", bufs=1))
 
         x_scale = keep.tile([P, T], U8, name="x_scale", align_bytes=64)
@@ -40,7 +44,10 @@ def tile_picked_widxput_min_lo_kernel(tc, x_words, x_scales, mem, w1, slot, out_
         out_rows = out_0.rearrange("(p t) u -> p t u", t=PACK)
         mem_of = [mem_even[0, :, 0, :], mem_even[1, :, 0, :], mem_rows[:, 1, :], mem_rows[:, 3, :]]
         out_of = [out_even[0, :, 0, :], out_even[1, :, 0, :], out_rows[:, 1, :], out_rows[:, 3, :]]
-        w_raw = [keep.tile([P, PACK, N // 2], F32, name=f"w_raw{a}") for a in range(2)]
+        w_raw = [
+            keep.tile([P, PACK, N // 2], F32, name="w_raw0"),
+            shared.tile([P, PACK, N // 2], F32, name="w_raw1", offset=0),
+        ]
         store = [keep.tile([P, U], F32, name=f"store{s}") for s in range(4)]
         offsets = keep.tile([P, T // 16], U16, name="offsets")
         x_codes = keep.tile([P, T], U32, name="x_codes", align_bytes=64)
@@ -49,8 +56,8 @@ def tile_picked_widxput_min_lo_kernel(tc, x_words, x_scales, mem, w1, slot, out_
         nc.sync.dma_start(store[0][:], mem_of[0])
         nc.sync.dma_start(x_codes[:].bitcast(I32), x_words[0].rearrange("p c r -> p (c r)").bitcast(I32))
         nc.sync.dma_start(store[1][:], mem_of[1])
-        nc.sync.dma_start(w_raw[1][:], w_rows[:, :, N // 2 : N])
         nc.sync.dma_start(store[2][:], mem_of[2])
+        nc.sync.dma_start(w_raw[1][:], w_rows[:, :, N // 2 : N])
         nc.sync.dma_start(store[3][:], mem_of[3])
 
         w_even = [keep.tile([P, P, PACK], BF16, name=f"w_even{a}", align_bytes=64) for a in range(2)]
@@ -65,8 +72,8 @@ def tile_picked_widxput_min_lo_kernel(tc, x_words, x_scales, mem, w1, slot, out_
                 w_raw[a][:].rearrange("p j (l h e) -> p l h e j", h=2, e=2)[:, :, :, 1, :],
             )
 
-        def quantise(grouped_w, width, name):
-            codes = keep.tile([P, width], U32, name=name + "_codes", align_bytes=64)
+        def quantise(grouped_w, width, name, slot_of=None):
+            codes = keep.tile([P, width], U32, name=name + "_codes", tag=(slot_of or name) + "_codes", align_bytes=64)
             scale = keep.tile([P, width], U8, name=name + "_scale", align_bytes=64)
             nc.vector.quantize_mx(out=codes[:].bitcast(FP8X4), scales=scale[:], in_=grouped_w)
             return codes, scale
@@ -85,19 +92,23 @@ def tile_picked_widxput_min_lo_kernel(tc, x_words, x_scales, mem, w1, slot, out_
             return bank
 
         starts = [sum(CHUNKS[:c]) for c in range(len(CHUNKS))]
-        grouped = [keep.tile([P, n, PACK], BF16, name=f"grouped{c}", align_bytes=64) for c, n in enumerate(CHUNKS)]
-        picked = {s: keep.tile([P, T], F32, name=f"picked{s}") for s in range(1, 4)}
-        moved = [keep.tile([P, 2, U // 2], F32, name=f"moved{g}") for g in range(2)]
+        grouped_row = keep.tile([P, U * PACK], BF16, name="grouped", align_bytes=64)
+        grouped = grouped_row[:].rearrange("p (c t) -> p c t", t=PACK)
+        picked = {}
+        moved = [keep.tile([P, 2, n], F32, name=f"moved{g}") for g, n in enumerate(MOVE_WIDTHS)]
+
+        move_starts = [sum(MOVE_WIDTHS[:g]) for g in range(len(MOVE_WIDTHS))]
 
         def move(a):
-            for g in range(2):
+            for g in range(len(MOVE_WIDTHS)):
                 for h in range(2):
                     nc.sync.dma_start(
-                        moved[g][a * HALF : (a + 1) * HALF, h, :], store[a][h:P:2, g * (U // 2) : (g + 1) * (U // 2)]
+                        moved[g][a * HALF : (a + 1) * HALF, h, :], store[a][h:P:2, move_starts[g] : move_starts[g] + MOVE_WIDTHS[g]]
                     )
             nc.sync.dma_start(out_of[a], store[a][:])
 
         def gather(s):
+            picked[s] = shared.tile([P, T], F32, name=f"picked{s}", offset=PICKED_AT[s])
             nc.vector.tensor_copy(picked[s][:], store[s][:].indirect(offsets[:]))
 
         def smaller(s, y):
@@ -109,48 +120,60 @@ def tile_picked_widxput_min_lo_kernel(tc, x_words, x_scales, mem, w1, slot, out_
         round_even(nc.vector.tensor_copy, 0)
         codes, scale = quantise(w_even[0][:].rearrange("p m j -> p (m j)"), P, "w_a")
         y_a = [project(codes, scale, 0, f"y_a{i}", i * (T // 2), T // 2) for i in range(2)]
-        round_even(nc.scalar.copy, 1)
         round_odd(0)
+        round_even(nc.scalar.copy, 1)
         round_odd(1)
 
-        first_picked = [keep.tile([P, T // 2], F32, name=f"first_picked{i}") for i in range(2)]
-        half_list = [offsets[:, i * (T // 32) : (i + 1) * (T // 32)] for i in range(2)]
+        half = T // 2
+        picked[0] = keep.tile([P, T], F32, name="picked0")
         for i in range(2):
-            nc.vector.tensor_copy(first_picked[i][:], store[0][:].indirect(half_list[i]))
+            nc.vector.tensor_copy(
+                picked[0][:, i * half : (i + 1) * half], store[0][:].indirect(offsets[:, i * half // 16 : (i + 1) * half // 16])
+            )
         for i in range(2):
-            nc.vector.tensor_tensor(first_picked[i][:], y_a[i][:], first_picked[i][:], MIN)
-        nc.vector.tensor_copy(store[0][:].indirect(half_list[0]), first_picked[0][:])
-        gather(1)
-        nc.vector.tensor_copy(store[0][:].indirect(half_list[1]), first_picked[1][:])
+            part = picked[0][:, i * half : (i + 1) * half]
+            nc.vector.tensor_tensor(part, y_a[i][:], part, MIN)
+        scatter(0)
         move(0)
         codes, scale = quantise(w_even[1][:].rearrange("p m j -> p (m j)"), P, "w_b")
         y_b = project(codes, scale, 0, "y_b")
-        gather(2)
-        smaller(1, y_b)
-        codes, scale = quantise(w_odd[:].rearrange("p h l j -> p (h l j)"), 2 * P, "w_odd")
-        y_odd = [project(codes, scale, h, f"y_odd{h}") for h in range(2)]
+        gather(1)
+        y_odd = []
+        codes, scale = quantise(w_odd[:, 0].rearrange("p l j -> p (l j)"), P, "w_c")
+        y_odd.append(project(codes, scale, 0, "y_c"))
+        gathered = picked[1]
+        picked[1] = shared.tile([P, T], F32, name="smaller1", offset=2048)
+        nc.vector.tensor_tensor(picked[1][:], y_b[:], gathered[:], MIN)
+        codes, scale = quantise(w_odd[:, 1].rearrange("p l j -> p (l j)"), P, "w_d", "w_b")
+        y_odd.append(project(codes, scale, 0, "y_d"))
         scatter(1)
         move(1)
-        for c, n in enumerate(CHUNKS):
-            g, first = divmod(starts[c], U // 2)
-            q, first = divmod(first, U // 4)
-            quarters = moved[g][:].rearrange("p h (q c) -> p c (h q)", q=2)
-            nc.scalar.copy(grouped[c][:, :, 0:3], quarters[:, first : first + n, q : q + 3])
+        for g in range(2):
+            nc.scalar.copy(
+                grouped[:, move_starts[g] : move_starts[g + 1], 0:PACK:2], moved[g][:].rearrange("p h c -> p c h")
+            )
+        seam = move_starts[2]
+        upper = grouped[:, seam:, :].rearrange("p (q c) t -> p q c t", q=2)
+        nc.scalar.copy(upper[:, :, 2 * SEAM :, 0:PACK:2], moved[2][:].rearrange("p h (q c) -> p q c h", q=2)[:, :, 2 * SEAM :, :])
+        quarters = moved[2][:].rearrange("p h (q c) -> p c (h q)", q=2)
+        for q in range(2):
+            nc.scalar.copy(upper[:, q, 0 : 2 * SEAM, 0:3], quarters[:, 0 : 2 * SEAM, q : q + 3])
 
+        gather(2)
         gather(3)
         smaller(2, y_odd[0])
         smaller(3, y_odd[1])
-        for h in range(2):
-            scatter(2 + h)
-            nc.sync.dma_start(out_of[2 + h], store[2 + h][:])
-            for c, n in enumerate(CHUNKS):
-                src = store[2 + h][:, starts[c] : starts[c] + n]
-                if h == 0:
-                    nc.scalar.copy(grouped[c][:, :, 1:PACK:2], src.unsqueeze(2).to_broadcast([P, n, 2]))
-                elif c < VECTOR_CHUNKS:
-                    nc.vector.tensor_copy(grouped[c][:, :, 3], src)
-                else:
-                    nc.scalar.copy(grouped[c][:, :, 3], src)
+        scatter(2)
+        nc.sync.dma_start(out_of[2], store[2][:])
+        for first, last in ((0, seam + SEAM), (seam + SEAM, 3 * U // 4 + SEAM), (3 * U // 4 + SEAM, U)):
+            nc.scalar.copy(
+                grouped[:, first:last, 1:PACK:2], store[2][:, first:last].unsqueeze(2).to_broadcast([P, last - first, 2])
+            )
+        scatter(3)
+        nc.sync.dma_start(out_of[3], store[3][:])
+        for c, n in enumerate(CHUNKS):
+            engine_copy = nc.vector.tensor_copy if c < VECTOR_CHUNKS else nc.scalar.copy
+            engine_copy(grouped[:, starts[c] : starts[c] + n, 3], store[3][:, starts[c] : starts[c] + n])
 
         words = out_1[0].rearrange("p c r -> p (c r)").bitcast(I32)
         o_scale = keep.tile([P, U], U8, name="o_scale", align_bytes=64)
@@ -162,7 +185,7 @@ def tile_picked_widxput_min_lo_kernel(tc, x_words, x_scales, mem, w1, slot, out_
                 nc.vector.quantize_mx(
                     out=o_codes[:, starts[c] - first : starts[c] - first + CHUNKS[c]].bitcast(FP8X4),
                     scales=o_scale[:, starts[c] : starts[c] + CHUNKS[c]],
-                    in_=grouped[c][:].rearrange("p c t -> p (c t)"),
+                    in_=grouped_row[:, PACK * starts[c] : PACK * (starts[c] + CHUNKS[c])],
                 )
             nc.sync.dma_start(words[:, first : first + width], o_codes[:].bitcast(I32))
         scale_rows = out_2[0].bitcast(I32)

@@ -56,8 +56,8 @@ def tile_picked_widxput_min_lo_kernel(tc, x_words, x_scales, mem, w1, slot, out_
         nc.sync.dma_start(store[0][:], mem_of[0])
         nc.sync.dma_start(x_codes[:].bitcast(I32), x_words[0].rearrange("p c r -> p (c r)").bitcast(I32))
         nc.sync.dma_start(store[1][:], mem_of[1])
-        nc.sync.dma_start(store[2][:], mem_of[2])
         nc.sync.dma_start(w_raw[1][:], w_rows[:, :, N // 2 : N])
+        nc.sync.dma_start(store[2][:], mem_of[2])
         nc.sync.dma_start(store[3][:], mem_of[3])
 
         w_even = [keep.tile([P, P, PACK], BF16, name=f"w_even{a}", align_bytes=64) for a in range(2)]

@@ -21,8 +21,8 @@ CHUNKS = (256, 256, 256, 128, 128)
 VECTOR_CHUNKS = 2
 MOVE_WIDTHS = (256, 256, 512)
 SEAM = 16
-PICKED_AT = {1: 0, 2: 0, 3: 2048}
-STORE_GROUPS = ((0,), (1, 2), (3, 4))
+PICKED_AT = {2: 3072, 3: 0}
+STORE_GROUPS = ((0, 1), (2, 3), (4,))
 
 
 def tile_picked_widxput_min_lo_kernel(tc, x_words, x_scales, mem, w1, slot, out_0, out_1, out_2):
@@ -50,11 +50,14 @@ def tile_picked_widxput_min_lo_kernel(tc, x_words, x_scales, mem, w1, slot, out_
         ]
         store = [keep.tile([P, U], F32, name=f"store{s}") for s in range(4)]
         offsets = keep.tile([P, T // 16], U16, name="offsets")
-        x_codes = keep.tile([P, T], U32, name="x_codes", align_bytes=64)
+        half = T // 2
+        x_codes = [keep.tile([P, half], U32, name=f"x_codes{i}", align_bytes=64) for i in range(2)]
+        x_rows = x_words[0].rearrange("p c r -> p (c r)").bitcast(I32)
         nc.sync.dma_start(w_raw[0][:], w_rows[:, :, 0 : N // 2])
         nc.sync.dma_start(offsets[:], slot)
         nc.sync.dma_start(store[0][:], mem_of[0])
-        nc.sync.dma_start(x_codes[:].bitcast(I32), x_words[0].rearrange("p c r -> p (c r)").bitcast(I32))
+        for i in range(2):
+            nc.sync.dma_start(x_codes[i][:].bitcast(I32), x_rows[:, i * half : (i + 1) * half])
         nc.sync.dma_start(store[1][:], mem_of[1])
         nc.sync.dma_start(w_raw[1][:], w_rows[:, :, N // 2 : N])
         nc.sync.dma_start(store[2][:], mem_of[2])
@@ -72,23 +75,33 @@ def tile_picked_widxput_min_lo_kernel(tc, x_words, x_scales, mem, w1, slot, out_
                 w_raw[a][:].rearrange("p j (l h e) -> p l h e j", h=2, e=2)[:, :, :, 1, :],
             )
 
-        def quantise(grouped_w, width, name, slot_of=None):
-            codes = keep.tile([P, width], U32, name=name + "_codes", tag=(slot_of or name) + "_codes", align_bytes=64)
+        def quantise(grouped_w, width, name):
+            codes = keep.tile([P, width], U32, name=name + "_codes", align_bytes=64)
             scale = keep.tile([P, width], U8, name=name + "_scale", align_bytes=64)
             nc.vector.quantize_mx(out=codes[:].bitcast(FP8X4), scales=scale[:], in_=grouped_w)
             return codes, scale
 
-        def project(codes, scale, e, name, first=0, width=T):
-            bank = psum.tile([P, width], F32, name=name)
+        def project(codes, scale, e, out, i):
             nc.tensor.matmul_mx(
-                out=bank[:],
+                out=out,
                 lhsT=codes[:, e * P : (e + 1) * P].bitcast(FP8X4),
                 lhsT_scale=scale[:, e * P : (e + 1) * P],
-                rhs=x_codes[:, first : first + width].bitcast(FP8X4),
-                rhs_scale=x_scale[:, first : first + width],
+                rhs=x_codes[i][:].bitcast(FP8X4),
+                rhs_scale=x_scale[:, i * half : (i + 1) * half],
                 start=True,
                 stop=True,
             )
+
+        def project_halves(codes, scale, name):
+            banks = [psum.tile([P, half], F32, name=f"{name}{i}") for i in range(2)]
+            for i in range(2):
+                project(codes, scale, 0, banks[i][:], i)
+            return banks
+
+        def project_whole(codes, scale, e, name):
+            bank = psum.tile([P, T], F32, name=name)
+            for i in range(2):
+                project(codes, scale, e, bank[:, i * half : (i + 1) * half], i)
             return bank
 
         starts = [sum(CHUNKS[:c]) for c in range(len(CHUNKS))]
@@ -119,12 +132,11 @@ def tile_picked_widxput_min_lo_kernel(tc, x_words, x_scales, mem, w1, slot, out_
 
         round_even(nc.vector.tensor_copy, 0)
         codes, scale = quantise(w_even[0][:].rearrange("p m j -> p (m j)"), P, "w_a")
-        y_a = [project(codes, scale, 0, f"y_a{i}", i * (T // 2), T // 2) for i in range(2)]
+        y_a = project_halves(codes, scale, "y_a")
         round_odd(0)
         round_even(nc.scalar.copy, 1)
         round_odd(1)
 
-        half = T // 2
         picked[0] = keep.tile([P, T], F32, name="picked0")
         for i in range(2):
             nc.vector.tensor_copy(
@@ -136,16 +148,17 @@ def tile_picked_widxput_min_lo_kernel(tc, x_words, x_scales, mem, w1, slot, out_
         scatter(0)
         move(0)
         codes, scale = quantise(w_even[1][:].rearrange("p m j -> p (m j)"), P, "w_b")
-        y_b = project(codes, scale, 0, "y_b")
-        gather(1)
-        y_odd = []
-        codes, scale = quantise(w_odd[:, 0].rearrange("p l j -> p (l j)"), P, "w_c")
-        y_odd.append(project(codes, scale, 0, "y_c"))
-        gathered = picked[1]
-        picked[1] = shared.tile([P, T], F32, name="smaller1", offset=2048)
-        nc.vector.tensor_tensor(picked[1][:], y_b[:], gathered[:], MIN)
-        codes, scale = quantise(w_odd[:, 1].rearrange("p l j -> p (l j)"), P, "w_d", "w_b")
-        y_odd.append(project(codes, scale, 0, "y_d"))
+        y_b = project_halves(codes, scale, "y_b")
+        gathered = [shared.tile([P, half], F32, name=f"gathered{i}", offset=2048 + 1024 * i) for i in range(2)]
+        picked[1] = shared.tile([P, T], F32, name="smaller1", offset=0)
+        for i in range(2):
+            nc.vector.tensor_copy(gathered[i][:], store[1][:].indirect(offsets[:, i * half // 16 : (i + 1) * half // 16]))
+        for i in range(2):
+            nc.vector.tensor_tensor(picked[1][:, i * half : (i + 1) * half], y_b[i][:], gathered[i][:], MIN)
+        codes = shared.tile([P, 2 * P], U32, name="w_odd_codes", offset=2048, align_bytes=64)
+        scale = keep.tile([P, 2 * P], U8, name="w_odd_scale", align_bytes=64)
+        nc.vector.quantize_mx(out=codes[:].bitcast(FP8X4), scales=scale[:], in_=w_odd[:].rearrange("p h l j -> p (h l j)"))
+        y_odd = [project_whole(codes, scale, h, f"y_odd{h}") for h in range(2)]
         scatter(1)
         move(1)
         for g in range(2):

@@ -21,7 +21,9 @@ CHUNKS = (256, 256, 256, 128, 128)
 VECTOR_CHUNKS = 2
 MOVE_WIDTHS = (256, 256, 512)
 SEAM = 16
-PICKED_AT = {2: 3072, 3: 0}
+PICKED_AT = {2: 512, 3: 2560}
+EARLY = 384
+PASSES = ((0, 256), (256, 384), (384, 512))
 STORE_GROUPS = ((0, 1), (2, 3), (4,))
 
 
@@ -46,20 +48,21 @@ def tile_picked_widxput_min_lo_kernel(tc, x_words, x_scales, mem, w1, slot, out_
         out_of = [out_even[0, :, 0, :], out_even[1, :, 0, :], out_rows[:, 1, :], out_rows[:, 3, :]]
         w_raw = [
             keep.tile([P, PACK, N // 2], F32, name="w_raw0"),
-            shared.tile([P, PACK, N // 2], F32, name="w_raw1", offset=0),
+            keep.tile([P, PACK, N // 2], F32, name="w_raw1"),
         ]
         store = [keep.tile([P, U], F32, name=f"store{s}") for s in range(4)]
         offsets = keep.tile([P, T // 16], U16, name="offsets")
         half = T // 2
-        x_codes = [keep.tile([P, half], U32, name=f"x_codes{i}", align_bytes=64) for i in range(2)]
+        x_early = keep.tile([P, EARLY], U32, name="x_early", align_bytes=64)
+        x_late = keep.tile([P, T - EARLY], U32, name="x_late", align_bytes=64)
         x_rows = x_words[0].rearrange("p c r -> p (c r)").bitcast(I32)
         nc.sync.dma_start(w_raw[0][:], w_rows[:, :, 0 : N // 2])
         nc.sync.dma_start(offsets[:], slot)
         nc.sync.dma_start(store[0][:], mem_of[0])
-        for i in range(2):
-            nc.sync.dma_start(x_codes[i][:].bitcast(I32), x_rows[:, i * half : (i + 1) * half])
-        nc.sync.dma_start(store[1][:], mem_of[1])
+        nc.sync.dma_start(x_early[:].bitcast(I32), x_rows[:, 0:EARLY])
         nc.sync.dma_start(w_raw[1][:], w_rows[:, :, N // 2 : N])
+        nc.sync.dma_start(store[1][:], mem_of[1])
+        nc.sync.dma_start(x_late[:].bitcast(I32), x_rows[:, EARLY:T])
         nc.sync.dma_start(store[2][:], mem_of[2])
         nc.sync.dma_start(store[3][:], mem_of[3])
 
@@ -75,34 +78,25 @@ def tile_picked_widxput_min_lo_kernel(tc, x_words, x_scales, mem, w1, slot, out_
                 w_raw[a][:].rearrange("p j (l h e) -> p l h e j", h=2, e=2)[:, :, :, 1, :],
             )
 
-        def quantise(grouped_w, width, name):
-            codes = keep.tile([P, width], U32, name=name + "_codes", align_bytes=64)
-            scale = keep.tile([P, width], U8, name=name + "_scale", align_bytes=64)
+        def quantise(grouped_w, codes, scale):
             nc.vector.quantize_mx(out=codes[:].bitcast(FP8X4), scales=scale[:], in_=grouped_w)
-            return codes, scale
 
-        def project(codes, scale, e, out, i):
-            nc.tensor.matmul_mx(
-                out=out,
-                lhsT=codes[:, e * P : (e + 1) * P].bitcast(FP8X4),
-                lhsT_scale=scale[:, e * P : (e + 1) * P],
-                rhs=x_codes[i][:].bitcast(FP8X4),
-                rhs_scale=x_scale[:, i * half : (i + 1) * half],
-                start=True,
-                stop=True,
-            )
-
-        def project_halves(codes, scale, name):
-            banks = [psum.tile([P, half], F32, name=f"{name}{i}") for i in range(2)]
-            for i in range(2):
-                project(codes, scale, 0, banks[i][:], i)
+        def project(codes, scale, count, first, last, name):
+            banks = [psum.tile([P, last - first], F32, name=f"{name}_{e}") for e in range(count)]
+            for lo, hi in PASSES:
+                if first <= lo and hi <= last:
+                    moving = x_early[:, lo:hi] if hi <= EARLY else x_late[:, lo - EARLY : hi - EARLY]
+                    for e in range(count):
+                        nc.tensor.matmul_mx(
+                            out=banks[e][:, lo - first : hi - first],
+                            lhsT=codes[:, e * P : (e + 1) * P].bitcast(FP8X4),
+                            lhsT_scale=scale[:, e * P : (e + 1) * P],
+                            rhs=moving.bitcast(FP8X4),
+                            rhs_scale=x_scale[:, lo:hi],
+                            start=True,
+                            stop=True,
+                        )
             return banks
-
-        def project_whole(codes, scale, e, name):
-            bank = psum.tile([P, T], F32, name=name)
-            for i in range(2):
-                project(codes, scale, e, bank[:, i * half : (i + 1) * half], i)
-            return bank
 
         starts = [sum(CHUNKS[:c]) for c in range(len(CHUNKS))]
         grouped_row = keep.tile([P, U * PACK], BF16, name="grouped", align_bytes=64)
@@ -130,35 +124,47 @@ def tile_picked_widxput_min_lo_kernel(tc, x_words, x_scales, mem, w1, slot, out_
         def scatter(s):
             nc.vector.tensor_copy(store[s][:].indirect(offsets[:]), picked[s][:])
 
+        def entries(first, last):
+            return offsets[:, first // 16 : last // 16]
+
         round_even(nc.vector.tensor_copy, 0)
-        codes, scale = quantise(w_even[0][:].rearrange("p m j -> p (m j)"), P, "w_a")
-        y_a = project_halves(codes, scale, "y_a")
+        codes_a = shared.tile([P, P], U32, name="w_a_codes", offset=5120, align_bytes=64)
+        scale_a = shared.tile([P, P], U8, name="w_a_scale", offset=3072, align_bytes=64)
+        quantise(w_even[0][:].rearrange("p m j -> p (m j)"), codes_a, scale_a)
+        y_a = [project(codes_a, scale_a, 1, lo, hi, f"y_a{lo}")[0] for lo, hi in PASSES]
         round_odd(0)
         round_even(nc.scalar.copy, 1)
         round_odd(1)
 
         picked[0] = keep.tile([P, T], F32, name="picked0")
-        for i in range(2):
-            nc.vector.tensor_copy(
-                picked[0][:, i * half : (i + 1) * half], store[0][:].indirect(offsets[:, i * half // 16 : (i + 1) * half // 16])
-            )
-        for i in range(2):
-            part = picked[0][:, i * half : (i + 1) * half]
+        for lo, hi in ((0, half), (half, T)):
+            nc.vector.tensor_copy(picked[0][:, lo:hi], store[0][:].indirect(entries(lo, hi)))
+
+        def smaller_first(i):
+            part = picked[0][:, PASSES[i][0] : PASSES[i][1]]
             nc.vector.tensor_tensor(part, y_a[i][:], part, MIN)
-        scatter(0)
-        move(0)
-        codes, scale = quantise(w_even[1][:].rearrange("p m j -> p (m j)"), P, "w_b")
-        y_b = project_halves(codes, scale, "y_b")
+
+        smaller_first(0)
+        smaller_first(1)
+        nc.vector.tensor_copy(store[0][:].indirect(entries(0, half)), picked[0][:, 0:half])
+        parts = ((0, half), (half, T))
         gathered = [shared.tile([P, half], F32, name=f"gathered{i}", offset=2048 + 1024 * i) for i in range(2)]
-        picked[1] = shared.tile([P, T], F32, name="smaller1", offset=0)
+        picked[1] = keep.tile([P, T], F32, name="smaller1")
+        nc.vector.tensor_copy(gathered[0][:], store[1][:].indirect(entries(*parts[0])))
+        smaller_first(2)
+        codes_b = shared.tile([P, P], U32, name="w_b_codes", offset=5120, align_bytes=64)
+        scale_b = keep.tile([P, P], U8, name="w_b_scale", align_bytes=64)
+        quantise(w_even[1][:].rearrange("p m j -> p (m j)"), codes_b, scale_b)
+        y_b = [project(codes_b, scale_b, 1, lo, hi, f"y_b{lo}")[0] for lo, hi in parts]
+        nc.vector.tensor_copy(gathered[1][:], store[1][:].indirect(entries(*parts[1])))
+        nc.vector.tensor_copy(store[0][:].indirect(entries(half, T)), picked[0][:, half:T])
+        move(0)
         for i in range(2):
-            nc.vector.tensor_copy(gathered[i][:], store[1][:].indirect(offsets[:, i * half // 16 : (i + 1) * half // 16]))
-        for i in range(2):
-            nc.vector.tensor_tensor(picked[1][:, i * half : (i + 1) * half], y_b[i][:], gathered[i][:], MIN)
-        codes = shared.tile([P, 2 * P], U32, name="w_odd_codes", offset=2048, align_bytes=64)
-        scale = keep.tile([P, 2 * P], U8, name="w_odd_scale", align_bytes=64)
-        nc.vector.quantize_mx(out=codes[:].bitcast(FP8X4), scales=scale[:], in_=w_odd[:].rearrange("p h l j -> p (h l j)"))
-        y_odd = [project_whole(codes, scale, h, f"y_odd{h}") for h in range(2)]
+            nc.vector.tensor_tensor(picked[1][:, parts[i][0] : parts[i][1]], y_b[i][:], gathered[i][:], MIN)
+        codes_odd = shared.tile([P, 2 * P], U32, name="w_odd_codes", offset=2048, align_bytes=64)
+        scale_odd = keep.tile([P, 2 * P], U8, name="w_odd_scale", align_bytes=64)
+        quantise(w_odd[:].rearrange("p h l j -> p (h l j)"), codes_odd, scale_odd)
+        y_odd = project(codes_odd, scale_odd, 2, 0, T, "y_odd")
         scatter(1)
         move(1)
         for g in range(2):

@@ -24,7 +24,7 @@ SEAM = 16
 PICKED_AT = {2: 512, 3: 2560}
 EARLY = 384
 PASSES = ((0, 256), (256, 384), (384, 512))
-STORE_GROUPS = ((0, 1), (2, 3), (4,))
+STORE_GROUPS = ((0,), (1,), (2,), (3, 4))
 
 
 def tile_picked_widxput_min_lo_kernel(tc, x_words, x_scales, mem, w1, slot, out_0, out_1, out_2):

@@ -22,8 +22,9 @@ VECTOR_CHUNKS = 2
 MOVE_WIDTHS = (256, 256, 512)
 SEAM = 16
 PICKED_AT = {2: 512, 3: 2560}
-EARLY = 384
-PASSES = ((0, 256), (256, 384), (384, 512))
+EARLY = 448
+PASSES = ((0, 256), (256, 384), (384, 448), (448, 512))
+FIRST_PARTS = ((0, 256), (256, 448), (448, 512))
 STORE_GROUPS = ((0,), (1,), (2,), (3, 4))
 
 
@@ -131,7 +132,7 @@ def tile_picked_widxput_min_lo_kernel(tc, x_words, x_scales, mem, w1, slot, out_
         codes_a = shared.tile([P, P], U32, name="w_a_codes", offset=5120, align_bytes=64)
         scale_a = shared.tile([P, P], U8, name="w_a_scale", offset=3072, align_bytes=64)
         quantise(w_even[0][:].rearrange("p m j -> p (m j)"), codes_a, scale_a)
-        y_a = [project(codes_a, scale_a, 1, lo, hi, f"y_a{lo}")[0] for lo, hi in PASSES]
+        y_a = [project(codes_a, scale_a, 1, lo, hi, f"y_a{lo}")[0] for lo, hi in FIRST_PARTS]
         round_odd(0)
         round_even(nc.scalar.copy, 1)
         round_odd(1)
@@ -141,7 +142,7 @@ def tile_picked_widxput_min_lo_kernel(tc, x_words, x_scales, mem, w1, slot, out_
             nc.vector.tensor_copy(picked[0][:, lo:hi], store[0][:].indirect(entries(lo, hi)))
 
         def smaller_first(i):
-            part = picked[0][:, PASSES[i][0] : PASSES[i][1]]
+            part = picked[0][:, FIRST_PARTS[i][0] : FIRST_PARTS[i][1]]
             nc.vector.tensor_tensor(part, y_a[i][:], part, MIN)
 
         smaller_first(0)

@@ -20,7 +20,8 @@ HALF = 64
 CHUNKS = (256, 256, 256, 128, 128)
 VECTOR_CHUNKS = 2
 MOVE_WIDTHS = (256, 256, 512)
-SEAM = 16
+MOVED_AT = (6144, 8192, 12288)
+LATE = 128
 PICKED_AT = {2: 512, 3: 2560}
 EARLY = 448
 PASSES = ((0, 256), (256, 384), (384, 448), (448, 512))
@@ -103,7 +104,7 @@ def tile_picked_widxput_min_lo_kernel(tc, x_words, x_scales, mem, w1, slot, out_
         grouped_row = keep.tile([P, U * PACK], BF16, name="grouped", align_bytes=64)
         grouped = grouped_row[:].rearrange("p (c t) -> p c t", t=PACK)
         picked = {}
-        moved = [keep.tile([P, 2, n], F32, name=f"moved{g}") for g, n in enumerate(MOVE_WIDTHS)]
+        moved = [shared.tile([P, 2, n], F32, name=f"moved{g}", offset=MOVED_AT[g]) for g, n in enumerate(MOVE_WIDTHS)]
 
         move_starts = [sum(MOVE_WIDTHS[:g]) for g in range(len(MOVE_WIDTHS))]
 
@@ -118,9 +119,6 @@ def tile_picked_widxput_min_lo_kernel(tc, x_words, x_scales, mem, w1, slot, out_
         def gather(s):
             picked[s] = shared.tile([P, T], F32, name=f"picked{s}", offset=PICKED_AT[s])
             nc.vector.tensor_copy(picked[s][:], store[s][:].indirect(offsets[:]))
-
-        def smaller(s, y):
-            nc.vector.tensor_tensor(picked[s][:], y[:], picked[s][:], MIN)
 
         def scatter(s):
             nc.vector.tensor_copy(store[s][:].indirect(offsets[:]), picked[s][:])
@@ -168,28 +166,26 @@ def tile_picked_widxput_min_lo_kernel(tc, x_words, x_scales, mem, w1, slot, out_
         y_odd = project(codes_odd, scale_odd, 2, 0, T, "y_odd")
         scatter(1)
         move(1)
-        for g in range(2):
+        for g, n in enumerate(MOVE_WIDTHS):
             nc.scalar.copy(
-                grouped[:, move_starts[g] : move_starts[g + 1], 0:PACK:2], moved[g][:].rearrange("p h c -> p c h")
+                grouped[:, move_starts[g] : move_starts[g] + n, 0:PACK:2], moved[g][:].rearrange("p h c -> p c h")
             )
-        seam = move_starts[2]
-        upper = grouped[:, seam:, :].rearrange("p (q c) t -> p q c t", q=2)
-        nc.scalar.copy(upper[:, :, 2 * SEAM :, 0:PACK:2], moved[2][:].rearrange("p h (q c) -> p q c h", q=2)[:, :, 2 * SEAM :, :])
-        quarters = moved[2][:].rearrange("p h (q c) -> p c (h q)", q=2)
-        for q in range(2):
-            nc.scalar.copy(upper[:, q, 0 : 2 * SEAM, 0:3], quarters[:, 0 : 2 * SEAM, q : q + 3])
 
+        cut = T - LATE
         gather(2)
-        gather(3)
-        smaller(2, y_odd[0])
-        smaller(3, y_odd[1])
-        scatter(2)
+        picked[3] = shared.tile([P, T], F32, name="picked3", offset=PICKED_AT[3])
+        nc.vector.tensor_copy(picked[3][:, 0:half], store[3][:].indirect(entries(0, half)))
+        nc.vector.tensor_tensor(picked[2][:, 0:cut], y_odd[0][:, 0:cut], picked[2][:, 0:cut], MIN)
+        nc.vector.tensor_copy(picked[3][:, half:T], store[3][:].indirect(entries(half, T)))
+        nc.vector.tensor_copy(store[2][:].indirect(entries(0, cut)), picked[2][:, 0:cut])
+        late2 = shared.tile([P, LATE], F32, name="late2", offset=MOVED_AT[1])
+        smaller3 = shared.tile([P, T], F32, name="smaller3", offset=MOVED_AT[1] + 4 * LATE)
+        nc.vector.tensor_tensor(late2[:], y_odd[0][:, cut:T], picked[2][:, cut:T], MIN)
+        nc.vector.tensor_tensor(smaller3[:], y_odd[1][:], picked[3][:], MIN)
+        nc.vector.tensor_copy(store[2][:].indirect(entries(cut, T)), late2[:])
         nc.sync.dma_start(out_of[2], store[2][:])
-        for first, last in ((0, seam + SEAM), (seam + SEAM, 3 * U // 4 + SEAM), (3 * U // 4 + SEAM, U)):
-            nc.scalar.copy(
-                grouped[:, first:last, 1:PACK:2], store[2][:, first:last].unsqueeze(2).to_broadcast([P, last - first, 2])
-            )
-        scatter(3)
+        nc.scalar.copy(grouped[:, :, 1], store[2][:])
+        nc.vector.tensor_copy(store[3][:].indirect(offsets[:]), smaller3[:])
         nc.sync.dma_start(out_of[3], store[3][:])
         for c, n in enumerate(CHUNKS):
             engine_copy = nc.vector.tensor_copy if c < VECTOR_CHUNKS else nc.scalar.copy

@@ -83,22 +83,24 @@ def tile_picked_widxput_min_lo_kernel(tc, x_words, x_scales, mem, w1, slot, out_
         def quantise(grouped_w, codes, scale):
             nc.vector.quantize_mx(out=codes[:].bitcast(FP8X4), scales=scale[:], in_=grouped_w)
 
-        def project(codes, scale, count, first, last, name):
-            banks = [psum.tile([P, last - first], F32, name=f"{name}_{e}") for e in range(count)]
+        def one_pass(bank, codes, scale, e, lo, hi):
+            moving = x_early[:, lo:hi] if hi <= EARLY else x_late[:, lo - EARLY : hi - EARLY]
+            nc.tensor.matmul_mx(
+                out=bank,
+                lhsT=codes[:, e * P : (e + 1) * P].bitcast(FP8X4),
+                lhsT_scale=scale[:, e * P : (e + 1) * P],
+                rhs=moving.bitcast(FP8X4),
+                rhs_scale=x_scale[:, lo:hi],
+                start=True,
+                stop=True,
+            )
+
+        def project(codes, scale, first, last, name):
+            bank = psum.tile([P, last - first], F32, name=name)
             for lo, hi in PASSES:
                 if first <= lo and hi <= last:
-                    moving = x_early[:, lo:hi] if hi <= EARLY else x_late[:, lo - EARLY : hi - EARLY]
-                    for e in range(count):
-                        nc.tensor.matmul_mx(
-                            out=banks[e][:, lo - first : hi - first],
-                            lhsT=codes[:, e * P : (e + 1) * P].bitcast(FP8X4),
-                            lhsT_scale=scale[:, e * P : (e + 1) * P],
-                            rhs=moving.bitcast(FP8X4),
-                            rhs_scale=x_scale[:, lo:hi],
-                            start=True,
-                            stop=True,
-                        )
-            return banks
+                    one_pass(bank[:, lo - first : hi - first], codes, scale, 0, lo, hi)
+            return bank
 
         starts = [sum(CHUNKS[:c]) for c in range(len(CHUNKS))]
         grouped_row = keep.tile([P, U * PACK], BF16, name="grouped", align_bytes=64)
@@ -130,7 +132,7 @@ def tile_picked_widxput_min_lo_kernel(tc, x_words, x_scales, mem, w1, slot, out_
         codes_a = shared.tile([P, P], U32, name="w_a_codes", offset=5120, align_bytes=64)
         scale_a = shared.tile([P, P], U8, name="w_a_scale", offset=3072, align_bytes=64)
         quantise(w_even[0][:].rearrange("p m j -> p (m j)"), codes_a, scale_a)
-        y_a = [project(codes_a, scale_a, 1, lo, hi, f"y_a{lo}")[0] for lo, hi in FIRST_PARTS]
+        y_a = [project(codes_a, scale_a, lo, hi, f"y_a{lo}") for lo, hi in FIRST_PARTS]
         round_odd(0)
         round_even(nc.scalar.copy, 1)
         round_odd(1)
@@ -154,7 +156,7 @@ def tile_picked_widxput_min_lo_kernel(tc, x_words, x_scales, mem, w1, slot, out_
         codes_b = shared.tile([P, P], U32, name="w_b_codes", offset=5120, align_bytes=64)
         scale_b = keep.tile([P, P], U8, name="w_b_scale", align_bytes=64)
         quantise(w_even[1][:].rearrange("p m j -> p (m j)"), codes_b, scale_b)
-        y_b = [project(codes_b, scale_b, 1, lo, hi, f"y_b{lo}")[0] for lo, hi in parts]
+        y_b = [project(codes_b, scale_b, lo, hi, f"y_b{lo}") for lo, hi in parts]
         nc.vector.tensor_copy(gathered[1][:], store[1][:].indirect(entries(*parts[1])))
         nc.vector.tensor_copy(store[0][:].indirect(entries(half, T)), picked[0][:, half:T])
         move(0)
@@ -163,29 +165,37 @@ def tile_picked_widxput_min_lo_kernel(tc, x_words, x_scales, mem, w1, slot, out_
         codes_odd = shared.tile([P, 2 * P], U32, name="w_odd_codes", offset=2048, align_bytes=64)
         scale_odd = keep.tile([P, 2 * P], U8, name="w_odd_scale", align_bytes=64)
         quantise(w_odd[:].rearrange("p h l j -> p (h l j)"), codes_odd, scale_odd)
-        y_odd = project(codes_odd, scale_odd, 2, 0, T, "y_odd")
+        cut = T - LATE
+        y_two = psum.tile([P, cut], F32, name="y_two")
+        y_three = psum.tile([P, half], F32, name="y_three")
+        y_late = psum.tile([P, LATE + half], F32, name="y_late")
+        for lo, hi in PASSES:
+            one_pass(y_two[:, lo:hi] if hi <= cut else y_late[:, lo - cut : hi - cut], codes_odd, scale_odd, 0, lo, hi)
+            one_pass(
+                y_three[:, lo:hi] if hi <= half else y_late[:, LATE + lo - half : LATE + hi - half],
+                codes_odd, scale_odd, 1, lo, hi,
+            )
         scatter(1)
         move(1)
+        late_sums = shared.tile([P, LATE + half], F32, name="late_sums", offset=MOVED_AT[1])
         for g, n in enumerate(MOVE_WIDTHS):
             nc.scalar.copy(
                 grouped[:, move_starts[g] : move_starts[g] + n, 0:PACK:2], moved[g][:].rearrange("p h c -> p c h")
             )
+            if g == 1:
+                nc.scalar.copy(late_sums[:], y_late[:])
 
-        cut = T - LATE
         gather(2)
-        picked[3] = shared.tile([P, T], F32, name="picked3", offset=PICKED_AT[3])
-        nc.vector.tensor_copy(picked[3][:, 0:half], store[3][:].indirect(entries(0, half)))
-        nc.vector.tensor_tensor(picked[2][:, 0:cut], y_odd[0][:, 0:cut], picked[2][:, 0:cut], MIN)
-        nc.vector.tensor_copy(picked[3][:, half:T], store[3][:].indirect(entries(half, T)))
+        gather(3)
+        nc.vector.tensor_tensor(picked[2][:, 0:cut], y_two[:], picked[2][:, 0:cut], MIN)
+        nc.vector.tensor_tensor(picked[3][:, 0:half], y_three[:], picked[3][:, 0:half], MIN)
         nc.vector.tensor_copy(store[2][:].indirect(entries(0, cut)), picked[2][:, 0:cut])
-        late2 = shared.tile([P, LATE], F32, name="late2", offset=MOVED_AT[1])
-        smaller3 = shared.tile([P, T], F32, name="smaller3", offset=MOVED_AT[1] + 4 * LATE)
-        nc.vector.tensor_tensor(late2[:], y_odd[0][:, cut:T], picked[2][:, cut:T], MIN)
-        nc.vector.tensor_tensor(smaller3[:], y_odd[1][:], picked[3][:], MIN)
-        nc.vector.tensor_copy(store[2][:].indirect(entries(cut, T)), late2[:])
+        nc.vector.tensor_tensor(picked[2][:, cut:T], late_sums[:, 0:LATE], picked[2][:, cut:T], MIN)
+        nc.vector.tensor_tensor(picked[3][:, half:T], late_sums[:, LATE:], picked[3][:, half:T], MIN)
+        nc.vector.tensor_copy(store[2][:].indirect(entries(cut, T)), picked[2][:, cut:T])
         nc.sync.dma_start(out_of[2], store[2][:])
         nc.scalar.copy(grouped[:, :, 1], store[2][:])
-        nc.vector.tensor_copy(store[3][:].indirect(offsets[:]), smaller3[:])
+        scatter(3)
         nc.sync.dma_start(out_of[3], store[3][:])
         for c, n in enumerate(CHUNKS):
             engine_copy = nc.vector.tensor_copy if c < VECTOR_CHUNKS else nc.scalar.copy

@@ -55,16 +55,15 @@ def tile_picked_widxput_min_lo_kernel(tc, x_words, x_scales, mem, w1, slot, out_
         store = [keep.tile([P, U], F32, name=f"store{s}") for s in range(4)]
         offsets = keep.tile([P, T // 16], U16, name="offsets")
         half = T // 2
-        x_early = keep.tile([P, EARLY], U32, name="x_early", align_bytes=64)
-        x_late = keep.tile([P, T - EARLY], U32, name="x_late", align_bytes=64)
+        x_codes = keep.tile([P, T], U32, name="x_codes", align_bytes=64)
         x_rows = x_words[0].rearrange("p c r -> p (c r)").bitcast(I32)
         nc.sync.dma_start(w_raw[0][:], w_rows[:, :, 0 : N // 2])
         nc.sync.dma_start(offsets[:], slot)
         nc.sync.dma_start(store[0][:], mem_of[0])
-        nc.sync.dma_start(x_early[:].bitcast(I32), x_rows[:, 0:EARLY])
+        nc.sync.dma_start(x_codes[:, 0:EARLY].bitcast(I32), x_rows[:, 0:EARLY])
         nc.sync.dma_start(w_raw[1][:], w_rows[:, :, N // 2 : N])
         nc.sync.dma_start(store[1][:], mem_of[1])
-        nc.sync.dma_start(x_late[:].bitcast(I32), x_rows[:, EARLY:T])
+        nc.sync.dma_start(x_codes[:, EARLY:T].bitcast(I32), x_rows[:, EARLY:T])
         nc.sync.dma_start(store[2][:], mem_of[2])
         nc.sync.dma_start(store[3][:], mem_of[3])
 
@@ -84,12 +83,11 @@ def tile_picked_widxput_min_lo_kernel(tc, x_words, x_scales, mem, w1, slot, out_
             nc.vector.quantize_mx(out=codes[:].bitcast(FP8X4), scales=scale[:], in_=grouped_w)
 
         def one_pass(bank, codes, scale, e, lo, hi):
-            moving = x_early[:, lo:hi] if hi <= EARLY else x_late[:, lo - EARLY : hi - EARLY]
             nc.tensor.matmul_mx(
                 out=bank,
                 lhsT=codes[:, e * P : (e + 1) * P].bitcast(FP8X4),
                 lhsT_scale=scale[:, e * P : (e + 1) * P],
-                rhs=moving.bitcast(FP8X4),
+                rhs=x_codes[:, lo:hi].bitcast(FP8X4),
                 rhs_scale=x_scale[:, lo:hi],
                 start=True,
                 stop=True,
@@ -156,7 +154,9 @@ def tile_picked_widxput_min_lo_kernel(tc, x_words, x_scales, mem, w1, slot, out_
         codes_b = shared.tile([P, P], U32, name="w_b_codes", offset=5120, align_bytes=64)
         scale_b = keep.tile([P, P], U8, name="w_b_scale", align_bytes=64)
         quantise(w_even[1][:].rearrange("p m j -> p (m j)"), codes_b, scale_b)
-        y_b = [project(codes_b, scale_b, lo, hi, f"y_b{lo}") for lo, hi in parts]
+        y_b = [psum.tile([P, half], F32, name=f"y_b{lo}") for lo, hi in parts]
+        for i, (lo, hi) in enumerate(parts):
+            one_pass(y_b[i][:], codes_b, scale_b, 0, lo, hi)
         nc.vector.tensor_copy(gathered[1][:], store[1][:].indirect(entries(*parts[1])))
         nc.vector.tensor_copy(store[0][:].indirect(entries(half, T)), picked[0][:, half:T])
         move(0)
@@ -169,12 +169,11 @@ def tile_picked_widxput_min_lo_kernel(tc, x_words, x_scales, mem, w1, slot, out_
         y_two = psum.tile([P, cut], F32, name="y_two")
         y_three = psum.tile([P, half], F32, name="y_three")
         y_late = psum.tile([P, LATE + half], F32, name="y_late")
-        for lo, hi in PASSES:
-            one_pass(y_two[:, lo:hi] if hi <= cut else y_late[:, lo - cut : hi - cut], codes_odd, scale_odd, 0, lo, hi)
-            one_pass(
-                y_three[:, lo:hi] if hi <= half else y_late[:, LATE + lo - half : LATE + hi - half],
-                codes_odd, scale_odd, 1, lo, hi,
-            )
+        one_pass(y_two[:, 0:half], codes_odd, scale_odd, 0, 0, half)
+        one_pass(y_two[:, half:cut], codes_odd, scale_odd, 0, half, cut)
+        one_pass(y_late[:, 0:LATE], codes_odd, scale_odd, 0, cut, T)
+        one_pass(y_three[:], codes_odd, scale_odd, 1, 0, half)
+        one_pass(y_late[:, LATE:], codes_odd, scale_odd, 1, half, T)
         scatter(1)
         move(1)
         late_sums = shared.tile([P, LATE + half], F32, name="late_sums", offset=MOVED_AT[1])

@@ -13,20 +13,15 @@ U16 = mybir.dt.uint16
 U8 = mybir.dt.uint8
 FP8X4 = mybir.dt.float8_e4m3fn_x4
 MIN = mybir.AluOpType.min
+COPY = mybir.ActivationFunctionType.Copy
 
 P = 128
 PACK = 4
-HALF = 64
-CHUNKS = (256, 256, 256, 128, 128)
-VECTOR_CHUNKS = 2
-MOVE_WIDTHS = (256, 256, 512)
-MOVED_AT = (6144, 8192, 12288)
-LATE = 128
-PICKED_AT = {2: 512, 3: 2560}
-EARLY = 448
-PASSES = ((0, 256), (256, 384), (384, 448), (448, 512))
-FIRST_PARTS = ((0, 256), (256, 448), (448, 512))
-STORE_GROUPS = ((0,), (1,), (2,), (3, 4))
+HALF = T // 2
+CHUNK = 256
+W_VECTOR = 44
+SCALAR_COLUMNS = 768
+VECTOR_ENTRIES = 384
 
 
 def tile_picked_widxput_min_lo_kernel(tc, x_words, x_scales, mem, w1, slot, out_0, out_1, out_2):
@@ -42,177 +37,121 @@ def tile_picked_widxput_min_lo_kernel(tc, x_words, x_scales, mem, w1, slot, out_
             nc.scalar.dma_start(x_scale[32 * q : 32 * q + 4, :].bitcast(I32), x_scale_rows[4 * q : 4 * q + 4, :])
 
         w_rows = w1.rearrange("(p j) c -> p j c", j=PACK)
-        mem_even = mem.rearrange("(a p e) u -> a p e u", a=2, e=2)
         mem_rows = mem.rearrange("(p t) u -> p t u", t=PACK)
-        out_even = out_0.rearrange("(a p e) u -> a p e u", a=2, e=2)
         out_rows = out_0.rearrange("(p t) u -> p t u", t=PACK)
-        mem_of = [mem_even[0, :, 0, :], mem_even[1, :, 0, :], mem_rows[:, 1, :], mem_rows[:, 3, :]]
-        out_of = [out_even[0, :, 0, :], out_even[1, :, 0, :], out_rows[:, 1, :], out_rows[:, 3, :]]
-        w_raw = [
-            keep.tile([P, PACK, N // 2], F32, name="w_raw0"),
-            keep.tile([P, PACK, N // 2], F32, name="w_raw1"),
-        ]
-        store = [keep.tile([P, U], F32, name=f"store{s}") for s in range(4)]
-        offsets = keep.tile([P, T // 16], U16, name="offsets")
-        half = T // 2
-        x_codes = keep.tile([P, T], U32, name="x_codes", align_bytes=64)
         x_rows = x_words[0].rearrange("p c r -> p (c r)").bitcast(I32)
+        w_raw = [keep.tile([P, PACK, N // 2], F32, name=f"w_raw{a}") for a in range(2)]
+        store = [keep.tile([P, U], F32, name=f"store{t}") for t in range(PACK)]
+        offsets = keep.tile([P, T // 16], U16, name="offsets")
+        x_codes = keep.tile([P, T], U32, name="x_codes", align_bytes=64)
         nc.sync.dma_start(w_raw[0][:], w_rows[:, :, 0 : N // 2])
-        nc.sync.dma_start(offsets[:], slot)
-        nc.sync.dma_start(store[0][:], mem_of[0])
-        nc.sync.dma_start(x_codes[:, 0:EARLY].bitcast(I32), x_rows[:, 0:EARLY])
         nc.sync.dma_start(w_raw[1][:], w_rows[:, :, N // 2 : N])
-        nc.sync.dma_start(store[1][:], mem_of[1])
-        nc.sync.dma_start(x_codes[:, EARLY:T].bitcast(I32), x_rows[:, EARLY:T])
-        nc.sync.dma_start(store[2][:], mem_of[2])
-        nc.sync.dma_start(store[3][:], mem_of[3])
+        nc.sync.dma_start(x_codes[:, 0:HALF].bitcast(I32), x_rows[:, 0:HALF])
+        nc.sync.dma_start(offsets[:], slot)
+        nc.sync.dma_start(store[0][:], mem_rows[:, 0, :])
+        nc.sync.dma_start(x_codes[:, HALF:T].bitcast(I32), x_rows[:, HALF:T])
+        for t in range(1, PACK):
+            nc.sync.dma_start(store[t][:], mem_rows[:, t, :])
 
-        w_even = [keep.tile([P, P, PACK], BF16, name=f"w_even{a}", align_bytes=64) for a in range(2)]
-        w_odd = keep.tile([P, 2, P, PACK], BF16, name="w_odd", align_bytes=64)
+        w_grouped = keep.tile([P, PACK * P * PACK], BF16, name="w_grouped", align_bytes=64)
+        w_dealt = w_grouped[:].rearrange("p (t m j) -> p m j t", t=PACK, j=PACK)
+        for a in range(2):
+            first = a * P // 2
+            source = w_raw[a][:].rearrange("p j (m t) -> p m j t", t=PACK)
+            nc.vector.tensor_copy(w_dealt[:, first : first + W_VECTOR, :, :], source[:, 0:W_VECTOR, :, :])
+            nc.scalar.activation(w_dealt[:, first + W_VECTOR : first + P // 2, :, :], source[:, W_VECTOR:, :, :], COPY)
+        w_codes = keep.tile([P, N], U32, name="w_codes", align_bytes=64)
+        w_scale = keep.tile([P, N], U8, name="w_scale", align_bytes=64)
 
-        def round_even(engine_copy, a):
-            engine_copy(w_even[a][:], w_raw[a][:].rearrange("p j (m e) -> p m e j", e=2)[:, :, 0, :])
-
-        def round_odd(a):
-            nc.scalar.copy(
-                w_odd[:, :, a * HALF : (a + 1) * HALF, :].rearrange("p h l j -> p l h j"),
-                w_raw[a][:].rearrange("p j (l h e) -> p l h e j", h=2, e=2)[:, :, :, 1, :],
+        def quantise_w(first, last):
+            nc.vector.quantize_mx(
+                out=w_codes[:, first * P : last * P].bitcast(FP8X4),
+                scales=w_scale[:, first * P : last * P],
+                in_=w_grouped[:, first * P * PACK : last * P * PACK],
             )
 
-        def quantise(grouped_w, codes, scale):
-            nc.vector.quantize_mx(out=codes[:].bitcast(FP8X4), scales=scale[:], in_=grouped_w)
-
-        def one_pass(bank, codes, scale, e, lo, hi):
+        def project(t, lo, hi):
+            bank = psum.tile([P, hi - lo], F32, name=f"y{t}_{lo}")
             nc.tensor.matmul_mx(
-                out=bank,
-                lhsT=codes[:, e * P : (e + 1) * P].bitcast(FP8X4),
-                lhsT_scale=scale[:, e * P : (e + 1) * P],
+                out=bank[:],
+                lhsT=w_codes[:, t * P : (t + 1) * P].bitcast(FP8X4),
+                lhsT_scale=w_scale[:, t * P : (t + 1) * P],
                 rhs=x_codes[:, lo:hi].bitcast(FP8X4),
                 rhs_scale=x_scale[:, lo:hi],
                 start=True,
                 stop=True,
             )
-
-        def project(codes, scale, first, last, name):
-            bank = psum.tile([P, last - first], F32, name=name)
-            for lo, hi in PASSES:
-                if first <= lo and hi <= last:
-                    one_pass(bank[:, lo - first : hi - first], codes, scale, 0, lo, hi)
             return bank
 
-        starts = [sum(CHUNKS[:c]) for c in range(len(CHUNKS))]
+        def entries(lo, hi):
+            return offsets[:, lo // 16 : hi // 16]
+
+        halves = ((0, HALF), (HALF, T))
+        last = PACK - 1
+        picked = [keep.tile([P, T], F32, name=f"picked{t}") for t in range(PACK)]
+        gathered = [
+            shared.tile([P, HALF], F32, name="gathered_a", offset=0),
+            keep.tile([P, HALF], F32, name="gathered_b"),
+        ]
+
+        def part(t, h):
+            return picked[t][:, halves[h][0] : halves[h][1]]
+
+        def old(t, h):
+            return gathered[h][:] if t == last else part(t, h)
+
+        quantise_w(0, 1)
+        y_first = [project(0, lo, hi) for lo, hi in halves]
+        quantise_w(1, 2)
+        quantise_w(2, 4)
+        y = [None] + [project(t, 0, T) for t in range(1, PACK)]
+
+        for h in range(2):
+            nc.scalar.activation(part(0, h), store[0][:].indirect(entries(*halves[h])), COPY)
+        for h in range(2):
+            nc.vector.tensor_tensor(part(0, h), y_first[h][:], part(0, h), MIN)
+        for t in range(1, PACK):
+            for h in range(2):
+                nc.vector.tensor_copy(old(t, h), store[t][:].indirect(entries(*halves[h])))
+            for h in range(2):
+                nc.vector.tensor_tensor(part(t, h), y[t][:, halves[h][0] : halves[h][1]], old(t, h), MIN)
+        for t in range(last):
+            for h in range(2):
+                nc.scalar.activation(store[t][:].indirect(entries(*halves[h])), part(t, h), COPY)
+            nc.sync.dma_start(out_rows[:, t, :], store[t][:])
+
+        pair_row = shared.tile([P, U * PACK], BF16, name="pairs", offset=0, align_bytes=64)
+        pairs = pair_row[:].rearrange("p (a c e) -> p a c e", a=2, e=2)
+        pair_words = pair_row[:].bitcast(F32).rearrange("p (a c) -> p c a", a=2)
+
+        def round_plane(t, lo, hi):
+            nc.vector.tensor_copy(pairs[:, t // 2, lo:hi, t % 2], store[t][:, lo:hi])
+
+        round_plane(0, 0, U)
+        nc.vector.tensor_copy(store[last][:].indirect(entries(0, VECTOR_ENTRIES)), picked[last][:, 0:VECTOR_ENTRIES])
+        round_plane(1, 0, U)
+        round_plane(2, 0, U)
+        nc.scalar.activation(store[last][:].indirect(entries(VECTOR_ENTRIES, T)), picked[last][:, VECTOR_ENTRIES:T], COPY)
+        nc.sync.dma_start(out_rows[:, last, :], store[last][:])
+
         grouped_row = keep.tile([P, U * PACK], BF16, name="grouped", align_bytes=64)
-        grouped = grouped_row[:].rearrange("p (c t) -> p c t", t=PACK)
-        picked = {}
-        moved = [shared.tile([P, 2, n], F32, name=f"moved{g}", offset=MOVED_AT[g]) for g, n in enumerate(MOVE_WIDTHS)]
-
-        move_starts = [sum(MOVE_WIDTHS[:g]) for g in range(len(MOVE_WIDTHS))]
-
-        def move(a):
-            for g in range(len(MOVE_WIDTHS)):
-                for h in range(2):
-                    nc.sync.dma_start(
-                        moved[g][a * HALF : (a + 1) * HALF, h, :], store[a][h:P:2, move_starts[g] : move_starts[g] + MOVE_WIDTHS[g]]
-                    )
-            nc.sync.dma_start(out_of[a], store[a][:])
-
-        def gather(s):
-            picked[s] = shared.tile([P, T], F32, name=f"picked{s}", offset=PICKED_AT[s])
-            nc.vector.tensor_copy(picked[s][:], store[s][:].indirect(offsets[:]))
-
-        def scatter(s):
-            nc.vector.tensor_copy(store[s][:].indirect(offsets[:]), picked[s][:])
-
-        def entries(first, last):
-            return offsets[:, first // 16 : last // 16]
-
-        round_even(nc.vector.tensor_copy, 0)
-        codes_a = shared.tile([P, P], U32, name="w_a_codes", offset=5120, align_bytes=64)
-        scale_a = shared.tile([P, P], U8, name="w_a_scale", offset=3072, align_bytes=64)
-        quantise(w_even[0][:].rearrange("p m j -> p (m j)"), codes_a, scale_a)
-        y_a = [project(codes_a, scale_a, lo, hi, f"y_a{lo}") for lo, hi in FIRST_PARTS]
-        round_odd(0)
-        round_even(nc.scalar.copy, 1)
-        round_odd(1)
-
-        picked[0] = keep.tile([P, T], F32, name="picked0")
-        for lo, hi in ((0, half), (half, T)):
-            nc.vector.tensor_copy(picked[0][:, lo:hi], store[0][:].indirect(entries(lo, hi)))
-
-        def smaller_first(i):
-            part = picked[0][:, FIRST_PARTS[i][0] : FIRST_PARTS[i][1]]
-            nc.vector.tensor_tensor(part, y_a[i][:], part, MIN)
-
-        smaller_first(0)
-        smaller_first(1)
-        nc.vector.tensor_copy(store[0][:].indirect(entries(0, half)), picked[0][:, 0:half])
-        parts = ((0, half), (half, T))
-        gathered = [shared.tile([P, half], F32, name=f"gathered{i}", offset=2048 + 1024 * i) for i in range(2)]
-        picked[1] = keep.tile([P, T], F32, name="smaller1")
-        nc.vector.tensor_copy(gathered[0][:], store[1][:].indirect(entries(*parts[0])))
-        smaller_first(2)
-        codes_b = shared.tile([P, P], U32, name="w_b_codes", offset=5120, align_bytes=64)
-        scale_b = keep.tile([P, P], U8, name="w_b_scale", align_bytes=64)
-        quantise(w_even[1][:].rearrange("p m j -> p (m j)"), codes_b, scale_b)
-        y_b = [psum.tile([P, half], F32, name=f"y_b{lo}") for lo, hi in parts]
-        for i, (lo, hi) in enumerate(parts):
-            one_pass(y_b[i][:], codes_b, scale_b, 0, lo, hi)
-        nc.vector.tensor_copy(gathered[1][:], store[1][:].indirect(entries(*parts[1])))
-        nc.vector.tensor_copy(store[0][:].indirect(entries(half, T)), picked[0][:, half:T])
-        move(0)
-        for i in range(2):
-            nc.vector.tensor_tensor(picked[1][:, parts[i][0] : parts[i][1]], y_b[i][:], gathered[i][:], MIN)
-        codes_odd = shared.tile([P, 2 * P], U32, name="w_odd_codes", offset=2048, align_bytes=64)
-        scale_odd = keep.tile([P, 2 * P], U8, name="w_odd_scale", align_bytes=64)
-        quantise(w_odd[:].rearrange("p h l j -> p (h l j)"), codes_odd, scale_odd)
-        cut = T - LATE
-        y_two = psum.tile([P, cut], F32, name="y_two")
-        y_three = psum.tile([P, half], F32, name="y_three")
-        y_late = psum.tile([P, LATE + half], F32, name="y_late")
-        one_pass(y_two[:, 0:half], codes_odd, scale_odd, 0, 0, half)
-        one_pass(y_two[:, half:cut], codes_odd, scale_odd, 0, half, cut)
-        one_pass(y_late[:, 0:LATE], codes_odd, scale_odd, 0, cut, T)
-        one_pass(y_three[:], codes_odd, scale_odd, 1, 0, half)
-        one_pass(y_late[:, LATE:], codes_odd, scale_odd, 1, half, T)
-        scatter(1)
-        move(1)
-        late_sums = shared.tile([P, LATE + half], F32, name="late_sums", offset=MOVED_AT[1])
-        for g, n in enumerate(MOVE_WIDTHS):
-            nc.scalar.copy(
-                grouped[:, move_starts[g] : move_starts[g] + n, 0:PACK:2], moved[g][:].rearrange("p h c -> p c h")
-            )
-            if g == 1:
-                nc.scalar.copy(late_sums[:], y_late[:])
-
-        gather(2)
-        gather(3)
-        nc.vector.tensor_tensor(picked[2][:, 0:cut], y_two[:], picked[2][:, 0:cut], MIN)
-        nc.vector.tensor_tensor(picked[3][:, 0:half], y_three[:], picked[3][:, 0:half], MIN)
-        nc.vector.tensor_copy(store[2][:].indirect(entries(0, cut)), picked[2][:, 0:cut])
-        nc.vector.tensor_tensor(picked[2][:, cut:T], late_sums[:, 0:LATE], picked[2][:, cut:T], MIN)
-        nc.vector.tensor_tensor(picked[3][:, half:T], late_sums[:, LATE:], picked[3][:, half:T], MIN)
-        nc.vector.tensor_copy(store[2][:].indirect(entries(cut, T)), picked[2][:, cut:T])
-        nc.sync.dma_start(out_of[2], store[2][:])
-        nc.scalar.copy(grouped[:, :, 1], store[2][:])
-        scatter(3)
-        nc.sync.dma_start(out_of[3], store[3][:])
-        for c, n in enumerate(CHUNKS):
-            engine_copy = nc.vector.tensor_copy if c < VECTOR_CHUNKS else nc.scalar.copy
-            engine_copy(grouped[:, starts[c] : starts[c] + n, 3], store[3][:, starts[c] : starts[c] + n])
+        grouped_words = grouped_row[:].bitcast(F32).rearrange("p (c a) -> p c a", a=2)
+        for lo in range(0, U, CHUNK):
+            round_plane(last, lo, lo + CHUNK)
+        for lo in range(0, U, CHUNK):
+            engine_copy = nc.scalar.copy if lo < SCALAR_COLUMNS else nc.vector.tensor_copy
+            engine_copy(grouped_words[:, lo : lo + CHUNK, :], pair_words[:, lo : lo + CHUNK, :])
 
         words = out_1[0].rearrange("p c r -> p (c r)").bitcast(I32)
         o_scale = keep.tile([P, U], U8, name="o_scale", align_bytes=64)
-        for g, group in enumerate(STORE_GROUPS):
-            first = starts[group[0]]
-            width = sum(CHUNKS[c] for c in group)
-            o_codes = keep.tile([P, width], U32, name=f"o_codes{g}", align_bytes=64)
-            for c in group:
-                nc.vector.quantize_mx(
-                    out=o_codes[:, starts[c] - first : starts[c] - first + CHUNKS[c]].bitcast(FP8X4),
-                    scales=o_scale[:, starts[c] : starts[c] + CHUNKS[c]],
-                    in_=grouped_row[:, PACK * starts[c] : PACK * (starts[c] + CHUNKS[c])],
-                )
-            nc.sync.dma_start(words[:, first : first + width], o_codes[:].bitcast(I32))
+        for lo in (0, 3 * CHUNK, CHUNK, 2 * CHUNK):
+            o_codes = keep.tile([P, CHUNK], U32, name=f"o_codes{lo}", align_bytes=64)
+            nc.vector.quantize_mx(
+                out=o_codes[:].bitcast(FP8X4),
+                scales=o_scale[:, lo : lo + CHUNK],
+                in_=grouped_row[:, PACK * lo : PACK * (lo + CHUNK)],
+            )
+            nc.sync.dma_start(words[:, lo : lo + CHUNK], o_codes[:].bitcast(I32))
         scale_rows = out_2[0].bitcast(I32)
         for q in range(4):
             queue = nc.scalar if q < 2 else nc.sync

@@ -13,6 +13,8 @@ U16 = mybir.dt.uint16
 U8 = mybir.dt.uint8
 FP8X4 = mybir.dt.float8_e4m3fn_x4
 MIN = mybir.AluOpType.min
+MULT = mybir.AluOpType.mult
+ADD = mybir.AluOpType.add
 COPY = mybir.ActivationFunctionType.Copy
 
 P = 128
@@ -21,7 +23,7 @@ HALF = T // 2
 CHUNK = 256
 W_VECTOR = 44
 SCALAR_COLUMNS = 768
-VECTOR_ENTRIES = 384
+VECTOR_ENTRIES = 128
 
 
 def tile_picked_widxput_min_lo_kernel(tc, x_words, x_scales, mem, w1, slot, out_0, out_1, out_2):
@@ -88,51 +90,72 @@ def tile_picked_widxput_min_lo_kernel(tc, x_words, x_scales, mem, w1, slot, out_
 
         halves = ((0, HALF), (HALF, T))
         last = PACK - 1
-        picked = [keep.tile([P, T], F32, name=f"picked{t}") for t in range(PACK)]
-        gathered = [
-            shared.tile([P, HALF], F32, name="gathered_a", offset=0),
-            keep.tile([P, HALF], F32, name="gathered_b"),
-        ]
+        own = PACK - 2
 
-        def part(t, h):
-            return picked[t][:, halves[h][0] : halves[h][1]]
+        def entries_of(h):
+            return entries(*halves[h])
 
-        def old(t, h):
-            return gathered[h][:] if t == last else part(t, h)
+        picked = {t: keep.tile([P, T], F32, name=f"picked{t}") for t in (0, 1, last)}
+        old = {(t, h): picked[t][:, halves[h][0] : halves[h][1]] for t in picked for h in range(2)}
+        old[last, 0] = shared.tile([P, HALF], F32, name="old_last", offset=0)[:]
+        for h in range(2):
+            old[own, h] = keep.tile([P, HALF], F32, name=f"old_own{h}")[:]
 
         quantise_w(0, 1)
-        y_first = [project(0, lo, hi) for lo, hi in halves]
+        y = {(0, h): project(0, *halves[h])[:] for h in range(2)}
         quantise_w(1, 2)
         quantise_w(2, 4)
-        y = [None] + [project(t, 0, T) for t in range(1, PACK)]
+        for t in (1, last, own):
+            bank = project(t, 0, T)
+            for h in range(2):
+                y[t, h] = bank[:, halves[h][0] : halves[h][1]]
 
-        for h in range(2):
-            nc.scalar.activation(part(0, h), store[0][:].indirect(entries(*halves[h])), COPY)
-        for h in range(2):
-            nc.vector.tensor_tensor(part(0, h), y_first[h][:], part(0, h), MIN)
-        for t in range(1, PACK):
+        def gather(t):
             for h in range(2):
-                nc.vector.tensor_copy(old(t, h), store[t][:].indirect(entries(*halves[h])))
-            for h in range(2):
-                nc.vector.tensor_tensor(part(t, h), y[t][:, halves[h][0] : halves[h][1]], old(t, h), MIN)
-        for t in range(last):
-            for h in range(2):
-                nc.scalar.activation(store[t][:].indirect(entries(*halves[h])), part(t, h), COPY)
-            nc.sync.dma_start(out_rows[:, t, :], store[t][:])
+                nc.vector.tensor_copy(old[t, h], store[t][:].indirect(entries_of(h)))
 
-        pair_row = shared.tile([P, U * PACK], BF16, name="pairs", offset=0, align_bytes=64)
+        def smaller(t, h):
+            nc.vector.tensor_tensor(picked[t][:, halves[h][0] : halves[h][1]], y[t, h], old[t, h], MIN)
+
+        def scatter_on_scalar(t, lo, hi):
+            nc.scalar.activation(store[t][:].indirect(entries(lo, hi)), picked[t][:, lo:hi], COPY)
+
+        def scatter_on_vector(t, lo, hi):
+            nc.vector.tensor_copy(store[t][:].indirect(entries(lo, hi)), picked[t][:, lo:hi])
+
+        nc.scalar.activation(old[0, 0], store[0][:].indirect(entries_of(0)), COPY)
+        nc.vector.tensor_copy(old[0, 1], store[0][:].indirect(entries_of(1)))
+        for h in range(2):
+            smaller(0, h)
+        gather(1)
+        for h in range(2):
+            smaller(1, h)
+        gather(own)
+        gather(last)
+        for h in range(2):
+            smaller(last, h)
+        picked[own] = shared.tile([P, T], F32, name="picked_own", offset=0)
+        for h in range(2):
+            smaller(own, h)
+
+        pair_row = keep.tile([P, U * PACK], BF16, name="pairs", align_bytes=64)
         pairs = pair_row[:].rearrange("p (a c e) -> p a c e", a=2, e=2)
         pair_words = pair_row[:].bitcast(F32).rearrange("p (a c) -> p c a", a=2)
 
         def round_plane(t, lo, hi):
             nc.vector.tensor_copy(pairs[:, t // 2, lo:hi, t % 2], store[t][:, lo:hi])
 
-        round_plane(0, 0, U)
-        nc.vector.tensor_copy(store[last][:].indirect(entries(0, VECTOR_ENTRIES)), picked[last][:, 0:VECTOR_ENTRIES])
-        round_plane(1, 0, U)
-        round_plane(2, 0, U)
-        nc.scalar.activation(store[last][:].indirect(entries(VECTOR_ENTRIES, T)), picked[last][:, VECTOR_ENTRIES:T], COPY)
-        nc.sync.dma_start(out_rows[:, last, :], store[last][:])
+        for t in range(2):
+            for lo, hi in halves:
+                scatter_on_scalar(t, lo, hi)
+            nc.sync.dma_start(out_rows[:, t, :], store[t][:])
+            nc.gpsimd.tensor_scalar(pairs[:, 0, :, t], store[t][:], 1.0, -0.0, MULT, ADD)
+        scatter_on_vector(last, 0, VECTOR_ENTRIES)
+        scatter_on_vector(own, 0, T)
+        nc.sync.dma_start(out_rows[:, own, :], store[own][:])
+        round_plane(own, 0, U)
+        scatter_on_scalar(last, VECTOR_ENTRIES, T)
+        nc.scalar.dma_start(out_rows[:, last, :], store[last][:])
 
         grouped_row = keep.tile([P, U * PACK], BF16, name="grouped", align_bytes=64)
         grouped_words = grouped_row[:].bitcast(F32).rearrange("p (c a) -> p c a", a=2)

@@ -21,7 +21,8 @@ P = 128
 PACK = 4
 HALF = T // 2
 CHUNK = 256
-W_VECTOR = 44
+W_VECTOR = 92
+FIRST = 128
 SCALAR_COLUMNS = 768
 VECTOR_ENTRIES = 128
 
@@ -42,12 +43,12 @@ def tile_picked_widxput_min_lo_kernel(tc, x_words, x_scales, mem, w1, slot, out_
         mem_rows = mem.rearrange("(p t) u -> p t u", t=PACK)
         out_rows = out_0.rearrange("(p t) u -> p t u", t=PACK)
         x_rows = x_words[0].rearrange("p c r -> p (c r)").bitcast(I32)
-        w_raw = [keep.tile([P, PACK, N // 2], F32, name=f"w_raw{a}") for a in range(2)]
+        w_raw = [keep.tile([P, PACK // 2, N], F32, name=f"w_raw{a}") for a in range(2)]
         store = [keep.tile([P, U], F32, name=f"store{t}") for t in range(PACK)]
         offsets = keep.tile([P, T // 16], U16, name="offsets")
         x_codes = keep.tile([P, T], U32, name="x_codes", align_bytes=64)
-        nc.sync.dma_start(w_raw[0][:], w_rows[:, :, 0 : N // 2])
-        nc.sync.dma_start(w_raw[1][:], w_rows[:, :, N // 2 : N])
+        nc.sync.dma_start(w_raw[0][:], w_rows[:, 0:2, :])
+        nc.sync.dma_start(w_raw[1][:], w_rows[:, 2:4, :])
         nc.sync.dma_start(x_codes[:, 0:HALF].bitcast(I32), x_rows[:, 0:HALF])
         nc.sync.dma_start(offsets[:], slot)
         nc.sync.dma_start(store[0][:], mem_rows[:, 0, :])
@@ -58,10 +59,9 @@ def tile_picked_widxput_min_lo_kernel(tc, x_words, x_scales, mem, w1, slot, out_
         w_grouped = keep.tile([P, PACK * P * PACK], BF16, name="w_grouped", align_bytes=64)
         w_dealt = w_grouped[:].rearrange("p (t m j) -> p m j t", t=PACK, j=PACK)
         for a in range(2):
-            first = a * P // 2
             source = w_raw[a][:].rearrange("p j (m t) -> p m j t", t=PACK)
-            nc.vector.tensor_copy(w_dealt[:, first : first + W_VECTOR, :, :], source[:, 0:W_VECTOR, :, :])
-            nc.scalar.activation(w_dealt[:, first + W_VECTOR : first + P // 2, :, :], source[:, W_VECTOR:, :, :], COPY)
+            nc.vector.tensor_copy(w_dealt[:, 0:W_VECTOR, 2 * a : 2 * a + 2, :], source[:, 0:W_VECTOR, :, :])
+            nc.scalar.activation(w_dealt[:, W_VECTOR:, 2 * a : 2 * a + 2, :], source[:, W_VECTOR:, :, :], COPY)
         w_codes = keep.tile([P, N], U32, name="w_codes", align_bytes=64)
         w_scale = keep.tile([P, N], U8, name="w_scale", align_bytes=64)
 
@@ -72,10 +72,9 @@ def tile_picked_widxput_min_lo_kernel(tc, x_words, x_scales, mem, w1, slot, out_
                 in_=w_grouped[:, first * P * PACK : last * P * PACK],
             )
 
-        def project(t, lo, hi):
-            bank = psum.tile([P, hi - lo], F32, name=f"y{t}_{lo}")
+        def one_pass(bank, t, lo, hi):
             nc.tensor.matmul_mx(
-                out=bank[:],
+                out=bank,
                 lhsT=w_codes[:, t * P : (t + 1) * P].bitcast(FP8X4),
                 lhsT_scale=w_scale[:, t * P : (t + 1) * P],
                 rhs=x_codes[:, lo:hi].bitcast(FP8X4),
@@ -83,39 +82,32 @@ def tile_picked_widxput_min_lo_kernel(tc, x_words, x_scales, mem, w1, slot, out_
                 start=True,
                 stop=True,
             )
-            return bank
 
         def entries(lo, hi):
             return offsets[:, lo // 16 : hi // 16]
 
-        halves = ((0, HALF), (HALF, T))
         last = PACK - 1
         own = PACK - 2
 
-        def entries_of(h):
-            return entries(*halves[h])
+        quantise_w(0, 1)
+        y_first = psum.tile([P, FIRST], F32, name="y_first")
+        one_pass(y_first[:], 0, 0, FIRST)
+        y = [psum.tile([P, T], F32, name=f"y{t}") for t in range(PACK)]
+        one_pass(y[0][:, FIRST:HALF], 0, FIRST, HALF)
+        one_pass(y[0][:, HALF:T], 0, HALF, T)
+        quantise_w(1, PACK)
+        for t in (1, last, own):
+            one_pass(y[t][:], t, 0, T)
 
         picked = {t: keep.tile([P, T], F32, name=f"picked{t}") for t in (0, 1, last)}
-        old = {(t, h): picked[t][:, halves[h][0] : halves[h][1]] for t in picked for h in range(2)}
-        old[last, 0] = shared.tile([P, HALF], F32, name="old_last", offset=0)[:]
-        for h in range(2):
-            old[own, h] = keep.tile([P, HALF], F32, name=f"old_own{h}")[:]
+        old_own = keep.tile([P, T], F32, name="old_own")
+        old_last = [shared.tile([P, HALF], F32, name=f"old_last{h}", offset=2048 * h) for h in range(2)]
 
-        quantise_w(0, 1)
-        y = {(0, h): project(0, *halves[h])[:] for h in range(2)}
-        quantise_w(1, 2)
-        quantise_w(2, 4)
-        for t in (1, last, own):
-            bank = project(t, 0, T)
-            for h in range(2):
-                y[t, h] = bank[:, halves[h][0] : halves[h][1]]
+        def gather(out, t, lo, hi):
+            nc.vector.tensor_copy(out, store[t][:].indirect(entries(lo, hi)))
 
-        def gather(t):
-            for h in range(2):
-                nc.vector.tensor_copy(old[t, h], store[t][:].indirect(entries_of(h)))
-
-        def smaller(t, h):
-            nc.vector.tensor_tensor(picked[t][:, halves[h][0] : halves[h][1]], y[t, h], old[t, h], MIN)
+        def smaller(t, lo, hi, sums, old):
+            nc.vector.tensor_tensor(picked[t][:, lo:hi], sums, old, MIN)
 
         def scatter_on_scalar(t, lo, hi):
             nc.scalar.activation(store[t][:].indirect(entries(lo, hi)), picked[t][:, lo:hi], COPY)
@@ -123,22 +115,25 @@ def tile_picked_widxput_min_lo_kernel(tc, x_words, x_scales, mem, w1, slot, out_
         def scatter_on_vector(t, lo, hi):
             nc.vector.tensor_copy(store[t][:].indirect(entries(lo, hi)), picked[t][:, lo:hi])
 
-        nc.scalar.activation(old[0, 0], store[0][:].indirect(entries_of(0)), COPY)
-        nc.vector.tensor_copy(old[0, 1], store[0][:].indirect(entries_of(1)))
-        for h in range(2):
-            smaller(0, h)
-        gather(1)
-        for h in range(2):
-            smaller(1, h)
-        gather(own)
-        gather(last)
-        for h in range(2):
-            smaller(last, h)
+        halves = ((0, HALF), (HALF, T))
+        nc.scalar.activation(picked[0][:, HALF:T], store[0][:].indirect(entries(HALF, T)), COPY)
+        gather(picked[0][:, 0:FIRST], 0, 0, FIRST)
+        gather(picked[0][:, FIRST:HALF], 0, FIRST, HALF)
+        smaller(0, 0, FIRST, y_first[:], picked[0][:, 0:FIRST])
+        smaller(0, FIRST, T, y[0][:, FIRST:T], picked[0][:, FIRST:T])
+        for lo, hi in halves:
+            gather(picked[1][:, lo:hi], 1, lo, hi)
+        for lo, hi in halves:
+            smaller(1, lo, hi, y[1][:, lo:hi], picked[1][:, lo:hi])
+        gather(old_own[:], own, 0, T)
+        for h, (lo, hi) in enumerate(halves):
+            gather(old_last[h][:], last, lo, hi)
+        for h, (lo, hi) in enumerate(halves):
+            smaller(last, lo, hi, y[last][:, lo:hi], old_last[h][:])
         picked[own] = shared.tile([P, T], F32, name="picked_own", offset=0)
-        for h in range(2):
-            smaller(own, h)
+        smaller(own, 0, T, y[own][:], old_own[:])
 
-        pair_row = keep.tile([P, U * PACK], BF16, name="pairs", align_bytes=64)
+        pair_row = shared.tile([P, U * PACK], BF16, name="pairs", offset=2048, align_bytes=64)
         pairs = pair_row[:].rearrange("p (a c e) -> p a c e", a=2, e=2)
         pair_words = pair_row[:].bitcast(F32).rearrange("p (a c) -> p c a", a=2)
 
@@ -146,8 +141,9 @@ def tile_picked_widxput_min_lo_kernel(tc, x_words, x_scales, mem, w1, slot, out_
             nc.vector.tensor_copy(pairs[:, t // 2, lo:hi, t % 2], store[t][:, lo:hi])
 
         for t in range(2):
-            for lo, hi in halves:
-                scatter_on_scalar(t, lo, hi)
+            cut = FIRST if t == 0 else HALF
+            scatter_on_scalar(t, 0, cut)
+            scatter_on_scalar(t, cut, T)
             nc.sync.dma_start(out_rows[:, t, :], store[t][:])
             nc.gpsimd.tensor_scalar(pairs[:, 0, :, t], store[t][:], 1.0, -0.0, MULT, ADD)
         scatter_on_vector(last, 0, VECTOR_ENTRIES)
@@ -159,8 +155,8 @@ def tile_picked_widxput_min_lo_kernel(tc, x_words, x_scales, mem, w1, slot, out_
 
         grouped_row = keep.tile([P, U * PACK], BF16, name="grouped", align_bytes=64)
         grouped_words = grouped_row[:].bitcast(F32).rearrange("p (c a) -> p c a", a=2)
-        for lo in range(0, U, CHUNK):
-            round_plane(last, lo, lo + CHUNK)
+        round_plane(last, 0, CHUNK)
+        round_plane(last, CHUNK, U)
         for lo in range(0, U, CHUNK):
             engine_copy = nc.scalar.copy if lo < SCALAR_COLUMNS else nc.vector.tensor_copy
             engine_copy(grouped_words[:, lo : lo + CHUNK, :], pair_words[:, lo : lo + CHUNK, :])

@@ -20,10 +20,11 @@ COPY = mybir.ActivationFunctionType.Copy
 P = 128
 PACK = 4
 HALF = T // 2
-CHUNK = 256
 W_VECTOR = 92
 FIRST = 128
-SCALAR_COLUMNS = 768
+SCALAR_ROUNDS = 256
+SCALAR_WORDS = 512
+STORED_PIECES = ((512, (768, 1024)), (0, (256,)), (256, (512,)))
 VECTOR_ENTRIES = 128
 
 
@@ -149,28 +150,32 @@ def tile_picked_widxput_min_lo_kernel(tc, x_words, x_scales, mem, w1, slot, out_
         scatter_on_vector(last, 0, VECTOR_ENTRIES)
         scatter_on_vector(own, 0, T)
         nc.sync.dma_start(out_rows[:, own, :], store[own][:])
-        round_plane(own, 0, U)
+        round_plane(own, SCALAR_ROUNDS, U)
         scatter_on_scalar(last, VECTOR_ENTRIES, T)
         nc.scalar.dma_start(out_rows[:, last, :], store[last][:])
 
         grouped_row = keep.tile([P, U * PACK], BF16, name="grouped", align_bytes=64)
         grouped_words = grouped_row[:].bitcast(F32).rearrange("p (c a) -> p c a", a=2)
-        round_plane(last, 0, CHUNK)
-        round_plane(last, CHUNK, U)
-        for lo in range(0, U, CHUNK):
-            engine_copy = nc.scalar.copy if lo < SCALAR_COLUMNS else nc.vector.tensor_copy
-            engine_copy(grouped_words[:, lo : lo + CHUNK, :], pair_words[:, lo : lo + CHUNK, :])
+        for t in (own, last):
+            nc.scalar.copy(pairs[:, 1, 0:SCALAR_ROUNDS, t % 2], store[t][:, 0:SCALAR_ROUNDS])
+        round_plane(last, SCALAR_WORDS, U)
+        round_plane(last, SCALAR_ROUNDS, SCALAR_WORDS)
+        for lo, hi in ((0, SCALAR_ROUNDS), (SCALAR_ROUNDS, SCALAR_WORDS)):
+            nc.scalar.copy(grouped_words[:, lo:hi, :], pair_words[:, lo:hi, :])
+        for lo, hi in ((SCALAR_WORDS, 768), (768, U)):
+            nc.vector.tensor_copy(grouped_words[:, lo:hi, :], pair_words[:, lo:hi, :])
 
         words = out_1[0].rearrange("p c r -> p (c r)").bitcast(I32)
         o_scale = keep.tile([P, U], U8, name="o_scale", align_bytes=64)
-        for lo in (0, 3 * CHUNK, CHUNK, 2 * CHUNK):
-            o_codes = keep.tile([P, CHUNK], U32, name=f"o_codes{lo}", align_bytes=64)
-            nc.vector.quantize_mx(
-                out=o_codes[:].bitcast(FP8X4),
-                scales=o_scale[:, lo : lo + CHUNK],
-                in_=grouped_row[:, PACK * lo : PACK * (lo + CHUNK)],
-            )
-            nc.sync.dma_start(words[:, lo : lo + CHUNK], o_codes[:].bitcast(I32))
+        for first, cuts in STORED_PIECES:
+            o_codes = keep.tile([P, cuts[-1] - first], U32, name=f"o_codes{first}", align_bytes=64)
+            for lo, hi in zip((first,) + cuts, cuts):
+                nc.vector.quantize_mx(
+                    out=o_codes[:, lo - first : hi - first].bitcast(FP8X4),
+                    scales=o_scale[:, lo:hi],
+                    in_=grouped_row[:, PACK * lo : PACK * hi],
+                )
+            nc.sync.dma_start(words[:, first : cuts[-1]], o_codes[:].bitcast(I32))
         scale_rows = out_2[0].bitcast(I32)
         for q in range(4):
             queue = nc.scalar if q < 2 else nc.sync

@@ -22,6 +22,8 @@ PACK = 4
 HALF = T // 2
 W_VECTOR = 92
 FIRST = 128
+EARLY = 224
+LATE_AT = 400
 SCALAR_ROUNDS = 256
 SCALAR_WORDS = 512
 STORED_PIECES = ((512, (768, 1024)), (0, (256,)), (256, (512,)))
@@ -32,7 +34,6 @@ def tile_picked_widxput_min_lo_kernel(tc, x_words, x_scales, mem, w1, slot, out_
     nc = tc.nc
     with ExitStack() as ctx:
         keep = ctx.enter_context(tc.tile_pool(name="keep", bufs=1))
-        shared = ctx.enter_context(tc.tile_pool(name="shared", bufs=1))
         psum = ctx.enter_context(tc.psum_pool(name="psum", bufs=1))
 
         x_scale = keep.tile([P, T], U8, name="x_scale", align_bytes=64)
@@ -54,7 +55,7 @@ def tile_picked_widxput_min_lo_kernel(tc, x_words, x_scales, mem, w1, slot, out_
         nc.sync.dma_start(offsets[:], slot)
         nc.sync.dma_start(store[0][:], mem_rows[:, 0, :])
         nc.sync.dma_start(x_codes[:, HALF:T].bitcast(I32), x_rows[:, HALF:T])
-        for t in range(1, PACK):
+        for t in (3, 1, 2):
             nc.sync.dma_start(store[t][:], mem_rows[:, t, :])
 
         w_grouped = keep.tile([P, PACK * P * PACK], BF16, name="w_grouped", align_bytes=64)
@@ -97,12 +98,15 @@ def tile_picked_widxput_min_lo_kernel(tc, x_words, x_scales, mem, w1, slot, out_
         one_pass(y[0][:, FIRST:HALF], 0, FIRST, HALF)
         one_pass(y[0][:, HALF:T], 0, HALF, T)
         quantise_w(1, PACK)
-        for t in (1, last, own):
+        for t in (last, 1, own):
             one_pass(y[t][:], t, 0, T)
 
-        picked = {t: keep.tile([P, T], F32, name=f"picked{t}") for t in (0, 1, last)}
-        old_own = keep.tile([P, T], F32, name="old_own")
-        old_last = [shared.tile([P, HALF], F32, name=f"old_last{h}", offset=2048 * h) for h in range(2)]
+        picked = {t: keep.tile([P, T], F32, name=f"picked{t}") for t in (0, 1, own)}
+        old_last = keep.tile([P, T], F32, name="old_last")
+        pair_row = keep.tile([P, U * PACK], BF16, name="pairs", align_bytes=64)
+        lent = pair_row[:].bitcast(F32)[:, U + LATE_AT :]
+        old_own = lent[:, 0:HALF]
+        late = lent[:, 0 : T - EARLY]
 
         def gather(out, t, lo, hi):
             nc.vector.tensor_copy(out, store[t][:].indirect(entries(lo, hi)))
@@ -110,8 +114,8 @@ def tile_picked_widxput_min_lo_kernel(tc, x_words, x_scales, mem, w1, slot, out_
         def smaller(t, lo, hi, sums, old):
             nc.vector.tensor_tensor(picked[t][:, lo:hi], sums, old, MIN)
 
-        def scatter_on_scalar(t, lo, hi):
-            nc.scalar.activation(store[t][:].indirect(entries(lo, hi)), picked[t][:, lo:hi], COPY)
+        def scatter_on_scalar(t, lo, hi, values):
+            nc.scalar.activation(store[t][:].indirect(entries(lo, hi)), values, COPY)
 
         def scatter_on_vector(t, lo, hi):
             nc.vector.tensor_copy(store[t][:].indirect(entries(lo, hi)), picked[t][:, lo:hi])
@@ -122,44 +126,48 @@ def tile_picked_widxput_min_lo_kernel(tc, x_words, x_scales, mem, w1, slot, out_
         gather(picked[0][:, FIRST:HALF], 0, FIRST, HALF)
         smaller(0, 0, FIRST, y_first[:], picked[0][:, 0:FIRST])
         smaller(0, FIRST, T, y[0][:, FIRST:T], picked[0][:, FIRST:T])
+        gather(old_last[:, 0:EARLY], last, 0, EARLY)
+        gather(old_last[:, EARLY:T], last, EARLY, T)
+        nc.vector.tensor_tensor(old_last[:, 0:EARLY], y[last][:, 0:EARLY], old_last[:, 0:EARLY], MIN)
         for lo, hi in halves:
             gather(picked[1][:, lo:hi], 1, lo, hi)
         for lo, hi in halves:
             smaller(1, lo, hi, y[1][:, lo:hi], picked[1][:, lo:hi])
-        gather(old_own[:], own, 0, T)
-        for h, (lo, hi) in enumerate(halves):
-            gather(old_last[h][:], last, lo, hi)
-        for h, (lo, hi) in enumerate(halves):
-            smaller(last, lo, hi, y[last][:, lo:hi], old_last[h][:])
-        picked[own] = shared.tile([P, T], F32, name="picked_own", offset=0)
-        smaller(own, 0, T, y[own][:], old_own[:])
+        scatter_on_vector(1, 0, VECTOR_ENTRIES)
+        gather(old_own, own, 0, HALF)
+        gather(picked[own][:, HALF:T], own, HALF, T)
+        smaller(own, 0, HALF, y[own][:, 0:HALF], old_own)
+        smaller(own, HALF, T, y[own][:, HALF:T], picked[own][:, HALF:T])
+        nc.vector.tensor_tensor(late, y[last][:, EARLY:T], old_last[:, EARLY:T], MIN)
+        scatter_on_vector(own, 0, T)
 
-        pair_row = shared.tile([P, U * PACK], BF16, name="pairs", offset=2048, align_bytes=64)
         pairs = pair_row[:].rearrange("p (a c e) -> p a c e", a=2, e=2)
         pair_words = pair_row[:].bitcast(F32).rearrange("p (a c) -> p c a", a=2)
 
         def round_plane(t, lo, hi):
             nc.vector.tensor_copy(pairs[:, t // 2, lo:hi, t % 2], store[t][:, lo:hi])
 
-        for t in range(2):
-            cut = FIRST if t == 0 else HALF
-            scatter_on_scalar(t, 0, cut)
-            scatter_on_scalar(t, cut, T)
+        def finish_early(t):
             nc.sync.dma_start(out_rows[:, t, :], store[t][:])
             nc.gpsimd.tensor_scalar(pairs[:, 0, :, t], store[t][:], 1.0, -0.0, MULT, ADD)
-        scatter_on_vector(last, 0, VECTOR_ENTRIES)
-        scatter_on_vector(own, 0, T)
+
+        scatter_on_scalar(0, 0, FIRST, picked[0][:, 0:FIRST])
+        scatter_on_scalar(0, FIRST, T, picked[0][:, FIRST:T])
+        finish_early(0)
+        scatter_on_scalar(last, 0, EARLY, old_last[:, 0:EARLY])
+        scatter_on_scalar(1, VECTOR_ENTRIES, T, picked[1][:, VECTOR_ENTRIES:T])
+        finish_early(1)
+        scatter_on_scalar(last, EARLY, T, late)
         nc.sync.dma_start(out_rows[:, own, :], store[own][:])
-        round_plane(own, SCALAR_ROUNDS, U)
-        scatter_on_scalar(last, VECTOR_ENTRIES, T)
         nc.scalar.dma_start(out_rows[:, last, :], store[last][:])
 
         grouped_row = keep.tile([P, U * PACK], BF16, name="grouped", align_bytes=64)
         grouped_words = grouped_row[:].bitcast(F32).rearrange("p (c a) -> p c a", a=2)
-        for t in (own, last):
+        for t in (last, own):
             nc.scalar.copy(pairs[:, 1, 0:SCALAR_ROUNDS, t % 2], store[t][:, 0:SCALAR_ROUNDS])
-        round_plane(last, SCALAR_WORDS, U)
-        round_plane(last, SCALAR_ROUNDS, SCALAR_WORDS)
+        round_plane(last, SCALAR_ROUNDS, U)
+        round_plane(own, SCALAR_WORDS, U)
+        round_plane(own, SCALAR_ROUNDS, SCALAR_WORDS)
         for lo, hi in ((0, SCALAR_ROUNDS), (SCALAR_ROUNDS, SCALAR_WORDS)):
             nc.scalar.copy(grouped_words[:, lo:hi, :], pair_words[:, lo:hi, :])
         for lo, hi in ((SCALAR_WORDS, 768), (768, U)):

@@ -22,10 +22,11 @@ PACK = 4
 HALF = T // 2
 W_VECTOR = 92
 FIRST = 128
-EARLY = 224
-LATE_AT = 400
-SCALAR_ROUNDS = 256
-SCALAR_WORDS = 512
+EARLY = 192
+LATE_AT = 640
+PIECE = 256
+SCALAR_ROUNDS = 384
+SCALAR_WORDS = 448
 STORED_PIECES = ((512, (768, 1024)), (0, (256,)), (256, (512,)))
 VECTOR_ENTRIES = 128
 
@@ -49,10 +50,10 @@ def tile_picked_widxput_min_lo_kernel(tc, x_words, x_scales, mem, w1, slot, out_
         store = [keep.tile([P, U], F32, name=f"store{t}") for t in range(PACK)]
         offsets = keep.tile([P, T // 16], U16, name="offsets")
         x_codes = keep.tile([P, T], U32, name="x_codes", align_bytes=64)
+        nc.sync.dma_start(offsets[:], slot)
         nc.sync.dma_start(w_raw[0][:], w_rows[:, 0:2, :])
         nc.sync.dma_start(w_raw[1][:], w_rows[:, 2:4, :])
         nc.sync.dma_start(x_codes[:, 0:HALF].bitcast(I32), x_rows[:, 0:HALF])
-        nc.sync.dma_start(offsets[:], slot)
         nc.sync.dma_start(store[0][:], mem_rows[:, 0, :])
         nc.sync.dma_start(x_codes[:, HALF:T].bitcast(I32), x_rows[:, HALF:T])
         for t in (3, 1, 2):
@@ -92,11 +93,10 @@ def tile_picked_widxput_min_lo_kernel(tc, x_words, x_scales, mem, w1, slot, out_
         own = PACK - 2
 
         quantise_w(0, 1)
-        y_first = psum.tile([P, FIRST], F32, name="y_first")
-        one_pass(y_first[:], 0, 0, FIRST)
-        y = [psum.tile([P, T], F32, name=f"y{t}") for t in range(PACK)]
-        one_pass(y[0][:, FIRST:HALF], 0, FIRST, HALF)
-        one_pass(y[0][:, HALF:T], 0, HALF, T)
+        y_first = [psum.tile([P, HALF], F32, name=f"y_first{h}") for h in range(2)]
+        one_pass(y_first[0][:], 0, 0, HALF)
+        one_pass(y_first[1][:], 0, HALF, T)
+        y = {t: psum.tile([P, T], F32, name=f"y{t}") for t in range(1, PACK)}
         quantise_w(1, PACK)
         for t in (last, 1, own):
             one_pass(y[t][:], t, 0, T)
@@ -124,8 +124,9 @@ def tile_picked_widxput_min_lo_kernel(tc, x_words, x_scales, mem, w1, slot, out_
         nc.scalar.activation(picked[0][:, HALF:T], store[0][:].indirect(entries(HALF, T)), COPY)
         gather(picked[0][:, 0:FIRST], 0, 0, FIRST)
         gather(picked[0][:, FIRST:HALF], 0, FIRST, HALF)
-        smaller(0, 0, FIRST, y_first[:], picked[0][:, 0:FIRST])
-        smaller(0, FIRST, T, y[0][:, FIRST:T], picked[0][:, FIRST:T])
+        smaller(0, 0, FIRST, y_first[0][:, 0:FIRST], picked[0][:, 0:FIRST])
+        smaller(0, FIRST, HALF, y_first[0][:, FIRST:HALF], picked[0][:, FIRST:HALF])
+        smaller(0, HALF, T, y_first[1][:], picked[0][:, HALF:T])
         gather(old_last[:, 0:EARLY], last, 0, EARLY)
         gather(old_last[:, EARLY:T], last, EARLY, T)
         nc.vector.tensor_tensor(old_last[:, 0:EARLY], y[last][:, 0:EARLY], old_last[:, 0:EARLY], MIN)
@@ -163,14 +164,14 @@ def tile_picked_widxput_min_lo_kernel(tc, x_words, x_scales, mem, w1, slot, out_
 
         grouped_row = keep.tile([P, U * PACK], BF16, name="grouped", align_bytes=64)
         grouped_words = grouped_row[:].bitcast(F32).rearrange("p (c a) -> p c a", a=2)
-        for t in (last, own):
-            nc.scalar.copy(pairs[:, 1, 0:SCALAR_ROUNDS, t % 2], store[t][:, 0:SCALAR_ROUNDS])
+        for t, lo, hi in ((last, 0, SCALAR_ROUNDS), (own, 0, PIECE), (own, PIECE, SCALAR_ROUNDS)):
+            nc.scalar.copy(pairs[:, 1, lo:hi, t % 2], store[t][:, lo:hi])
         round_plane(last, SCALAR_ROUNDS, U)
-        round_plane(own, SCALAR_WORDS, U)
-        round_plane(own, SCALAR_ROUNDS, SCALAR_WORDS)
-        for lo, hi in ((0, SCALAR_ROUNDS), (SCALAR_ROUNDS, SCALAR_WORDS)):
+        round_plane(own, SCALAR_ROUNDS, U - PIECE)
+        round_plane(own, U - PIECE, U)
+        for lo, hi in ((0, PIECE), (PIECE, SCALAR_WORDS)):
             nc.scalar.copy(grouped_words[:, lo:hi, :], pair_words[:, lo:hi, :])
-        for lo, hi in ((SCALAR_WORDS, 768), (768, U)):
+        for lo, hi in ((SCALAR_WORDS, U - PIECE), (U - PIECE, U)):
             nc.vector.tensor_copy(grouped_words[:, lo:hi, :], pair_words[:, lo:hi, :])
 
         words = out_1[0].rearrange("p c r -> p (c r)").bitcast(I32)

@@ -27,7 +27,7 @@ LATE_AT = 640
 PIECE = 256
 SCALAR_ROUNDS = 384
 SCALAR_WORDS = 448
-STORED_PIECES = ((512, (768, 1024)), (0, (256,)), (256, (512,)))
+STORED_PIECES = ((512, (768, 1024)), (0, (256, 512)))
 VECTOR_ENTRIES = 128
 
 

@@ -23,11 +23,11 @@ HALF = T // 2
 W_VECTOR = 92
 FIRST = 128
 EARLY = 192
-LATE_AT = 640
+LENT_AT = 512
 PIECE = 256
 SCALAR_ROUNDS = 384
 SCALAR_WORDS = 448
-STORED_PIECES = ((512, (768, 1024)), (0, (256, 512)))
+STORED_PIECES = ((512, (768, 1024)), (0, (256,)), (256, (512,)))
 VECTOR_ENTRIES = 128
 
 
@@ -55,8 +55,9 @@ def tile_picked_widxput_min_lo_kernel(tc, x_words, x_scales, mem, w1, slot, out_
         nc.sync.dma_start(w_raw[1][:], w_rows[:, 2:4, :])
         nc.sync.dma_start(x_codes[:, 0:HALF].bitcast(I32), x_rows[:, 0:HALF])
         nc.sync.dma_start(store[0][:], mem_rows[:, 0, :])
+        nc.sync.dma_start(store[3][:], mem_rows[:, 3, :])
         nc.sync.dma_start(x_codes[:, HALF:T].bitcast(I32), x_rows[:, HALF:T])
-        for t in (3, 1, 2):
+        for t in (1, 2):
             nc.sync.dma_start(store[t][:], mem_rows[:, t, :])
 
         w_grouped = keep.tile([P, PACK * P * PACK], BF16, name="w_grouped", align_bytes=64)
@@ -93,20 +94,21 @@ def tile_picked_widxput_min_lo_kernel(tc, x_words, x_scales, mem, w1, slot, out_
         own = PACK - 2
 
         quantise_w(0, 1)
-        y_first = [psum.tile([P, HALF], F32, name=f"y_first{h}") for h in range(2)]
-        one_pass(y_first[0][:], 0, 0, HALF)
-        one_pass(y_first[1][:], 0, HALF, T)
-        y = {t: psum.tile([P, T], F32, name=f"y{t}") for t in range(1, PACK)}
+        y_half = {(t, h): psum.tile([P, HALF], F32, name=f"y_half{t}{h}") for t in (0, last) for h in range(2)}
+        y = {t: psum.tile([P, T], F32, name=f"y{t}") for t in (1, own)}
+        one_pass(y_half[0, 0][:], 0, 0, HALF)
         quantise_w(1, PACK)
-        for t in (last, 1, own):
+        one_pass(y_half[last, 0][:], last, 0, HALF)
+        one_pass(y_half[0, 1][:], 0, HALF, T)
+        one_pass(y_half[last, 1][:], last, HALF, T)
+        for t in (1, own):
             one_pass(y[t][:], t, 0, T)
 
         picked = {t: keep.tile([P, T], F32, name=f"picked{t}") for t in (0, 1, own)}
         old_last = keep.tile([P, T], F32, name="old_last")
         pair_row = keep.tile([P, U * PACK], BF16, name="pairs", align_bytes=64)
-        lent = pair_row[:].bitcast(F32)[:, U + LATE_AT :]
-        old_own = lent[:, 0:HALF]
-        late = lent[:, 0 : T - EARLY]
+        lent = pair_row[:].bitcast(F32)[:, U + LENT_AT :]
+        old_own = lent[:, HALF:T]
 
         def gather(out, t, lo, hi):
             nc.vector.tensor_copy(out, store[t][:].indirect(entries(lo, hi)))
@@ -121,15 +123,15 @@ def tile_picked_widxput_min_lo_kernel(tc, x_words, x_scales, mem, w1, slot, out_
             nc.vector.tensor_copy(store[t][:].indirect(entries(lo, hi)), picked[t][:, lo:hi])
 
         halves = ((0, HALF), (HALF, T))
-        nc.scalar.activation(picked[0][:, HALF:T], store[0][:].indirect(entries(HALF, T)), COPY)
-        gather(picked[0][:, 0:FIRST], 0, 0, FIRST)
-        gather(picked[0][:, FIRST:HALF], 0, FIRST, HALF)
-        smaller(0, 0, FIRST, y_first[0][:, 0:FIRST], picked[0][:, 0:FIRST])
-        smaller(0, FIRST, HALF, y_first[0][:, FIRST:HALF], picked[0][:, FIRST:HALF])
-        smaller(0, HALF, T, y_first[1][:], picked[0][:, HALF:T])
-        gather(old_last[:, 0:EARLY], last, 0, EARLY)
-        gather(old_last[:, EARLY:T], last, EARLY, T)
-        nc.vector.tensor_tensor(old_last[:, 0:EARLY], y[last][:, 0:EARLY], old_last[:, 0:EARLY], MIN)
+        for lo, hi in ((FIRST, HALF), (HALF + FIRST, T)):
+            nc.scalar.activation(picked[0][:, lo:hi], store[0][:].indirect(entries(lo, hi)), COPY)
+        for lo in (0, HALF):
+            gather(picked[0][:, lo : lo + FIRST], 0, lo, lo + FIRST)
+        smaller(0, 0, HALF, y_half[0, 0][:], picked[0][:, 0:HALF])
+        for lo, hi in halves:
+            gather(old_last[:, lo:hi], last, lo, hi)
+        nc.vector.tensor_tensor(lent[:, 0:HALF], y_half[last, 0][:], old_last[:, 0:HALF], MIN)
+        smaller(0, HALF, T, y_half[0, 1][:], picked[0][:, HALF:T])
         for lo, hi in halves:
             gather(picked[1][:, lo:hi], 1, lo, hi)
         for lo, hi in halves:
@@ -139,7 +141,7 @@ def tile_picked_widxput_min_lo_kernel(tc, x_words, x_scales, mem, w1, slot, out_
         gather(picked[own][:, HALF:T], own, HALF, T)
         smaller(own, 0, HALF, y[own][:, 0:HALF], old_own)
         smaller(own, HALF, T, y[own][:, HALF:T], picked[own][:, HALF:T])
-        nc.vector.tensor_tensor(late, y[last][:, EARLY:T], old_last[:, EARLY:T], MIN)
+        nc.vector.tensor_tensor(lent[:, HALF:T], y_half[last, 1][:], old_last[:, HALF:T], MIN)
         scatter_on_vector(own, 0, T)
 
         pairs = pair_row[:].rearrange("p (a c e) -> p a c e", a=2, e=2)
@@ -152,15 +154,15 @@ def tile_picked_widxput_min_lo_kernel(tc, x_words, x_scales, mem, w1, slot, out_
             nc.sync.dma_start(out_rows[:, t, :], store[t][:])
             nc.gpsimd.tensor_scalar(pairs[:, 0, :, t], store[t][:], 1.0, -0.0, MULT, ADD)
 
-        scatter_on_scalar(0, 0, FIRST, picked[0][:, 0:FIRST])
-        scatter_on_scalar(0, FIRST, T, picked[0][:, FIRST:T])
+        scatter_on_scalar(0, 0, HALF, picked[0][:, 0:HALF])
+        scatter_on_scalar(last, 0, EARLY, lent[:, 0:EARLY])
+        scatter_on_scalar(0, HALF, T, picked[0][:, HALF:T])
         finish_early(0)
-        scatter_on_scalar(last, 0, EARLY, old_last[:, 0:EARLY])
         scatter_on_scalar(1, VECTOR_ENTRIES, T, picked[1][:, VECTOR_ENTRIES:T])
         finish_early(1)
-        scatter_on_scalar(last, EARLY, T, late)
-        nc.sync.dma_start(out_rows[:, own, :], store[own][:])
-        nc.scalar.dma_start(out_rows[:, last, :], store[last][:])
+        scatter_on_scalar(last, EARLY, T, lent[:, EARLY:T])
+        for t in (last, own):
+            nc.sync.dma_start(out_rows[:, t, :], store[t][:])
 
         grouped_row = keep.tile([P, U * PACK], BF16, name="grouped", align_bytes=64)
         grouped_words = grouped_row[:].bitcast(F32).rearrange("p (c a) -> p c a", a=2)

@@ -22,11 +22,12 @@ PACK = 4
 HALF = T // 2
 W_VECTOR = 92
 FIRST = 128
-EARLY = 192
-LENT_AT = 512
+EARLY = 128
+LATE = T - EARLY
+SCALAR_GATHERS = 128
 PIECE = 256
 SCALAR_ROUNDS = 384
-SCALAR_WORDS = 448
+SCALAR_WORDS = 512
 STORED_PIECES = ((512, (768, 1024)), (0, (256,)), (256, (512,)))
 VECTOR_ENTRIES = 128
 
@@ -94,21 +95,25 @@ def tile_picked_widxput_min_lo_kernel(tc, x_words, x_scales, mem, w1, slot, out_
         own = PACK - 2
 
         quantise_w(0, 1)
-        y_half = {(t, h): psum.tile([P, HALF], F32, name=f"y_half{t}{h}") for t in (0, last) for h in range(2)}
+        y_first = [psum.tile([P, HALF], F32, name=f"y_first{h}") for h in range(2)]
+        y_early = psum.tile([P, EARLY], F32, name="y_early")
+        y_late = psum.tile([P, LATE], F32, name="y_late")
         y = {t: psum.tile([P, T], F32, name=f"y{t}") for t in (1, own)}
-        one_pass(y_half[0, 0][:], 0, 0, HALF)
+        one_pass(y_first[0][:], 0, 0, HALF)
         quantise_w(1, PACK)
-        one_pass(y_half[last, 0][:], last, 0, HALF)
-        one_pass(y_half[0, 1][:], 0, HALF, T)
-        one_pass(y_half[last, 1][:], last, HALF, T)
+        one_pass(y_first[1][:], 0, HALF, T)
+        one_pass(y_early[:], last, LATE, T)
+        for lo, hi in ((0, HALF), (HALF, LATE)):
+            one_pass(y_late[:, lo:hi], last, lo, hi)
         for t in (1, own):
             one_pass(y[t][:], t, 0, T)
 
         picked = {t: keep.tile([P, T], F32, name=f"picked{t}") for t in (0, 1, own)}
         old_last = keep.tile([P, T], F32, name="old_last")
         pair_row = keep.tile([P, U * PACK], BF16, name="pairs", align_bytes=64)
-        lent = pair_row[:].bitcast(F32)[:, U + LENT_AT :]
-        old_own = lent[:, HALF:T]
+        new_last = keep.tile([P, T], F32, name="new_last")
+        old_second = keep.tile([P, HALF], F32, name="old_second")
+        old_halves = (new_last[:, 0:HALF], old_second[:])
 
         def gather(out, t, lo, hi):
             nc.vector.tensor_copy(out, store[t][:].indirect(entries(lo, hi)))
@@ -127,21 +132,19 @@ def tile_picked_widxput_min_lo_kernel(tc, x_words, x_scales, mem, w1, slot, out_
             nc.scalar.activation(picked[0][:, lo:hi], store[0][:].indirect(entries(lo, hi)), COPY)
         for lo in (0, HALF):
             gather(picked[0][:, lo : lo + FIRST], 0, lo, lo + FIRST)
-        smaller(0, 0, HALF, y_half[0, 0][:], picked[0][:, 0:HALF])
-        for lo, hi in halves:
-            gather(old_last[:, lo:hi], last, lo, hi)
-        nc.vector.tensor_tensor(lent[:, 0:HALF], y_half[last, 0][:], old_last[:, 0:HALF], MIN)
-        smaller(0, HALF, T, y_half[0, 1][:], picked[0][:, HALF:T])
-        for lo, hi in halves:
-            gather(picked[1][:, lo:hi], 1, lo, hi)
-        for lo, hi in halves:
-            smaller(1, lo, hi, y[1][:, lo:hi], picked[1][:, lo:hi])
-        scatter_on_vector(1, 0, VECTOR_ENTRIES)
-        gather(old_own, own, 0, HALF)
-        gather(picked[own][:, HALF:T], own, HALF, T)
-        smaller(own, 0, HALF, y[own][:, 0:HALF], old_own)
-        smaller(own, HALF, T, y[own][:, HALF:T], picked[own][:, HALF:T])
-        nc.vector.tensor_tensor(lent[:, HALF:T], y_half[last, 1][:], old_last[:, HALF:T], MIN)
+        smaller(0, 0, HALF, y_first[0][:], picked[0][:, 0:HALF])
+        nc.scalar.activation(old_last[:, 0:SCALAR_GATHERS], store[last][:].indirect(entries(0, SCALAR_GATHERS)), COPY)
+        gather(old_last[:, SCALAR_GATHERS:T], last, SCALAR_GATHERS, T)
+        smaller(0, HALF, T, y_first[1][:], picked[0][:, HALF:T])
+        nc.vector.tensor_tensor(new_last[:, LATE:T], y_early[:], old_last[:, LATE:T], MIN)
+        for t in (1, own):
+            for old, (lo, hi) in zip(old_halves, halves):
+                gather(old, t, lo, hi)
+            for old, (lo, hi) in zip(old_halves, halves):
+                smaller(t, lo, hi, y[t][:, lo:hi], old)
+            if t == 1:
+                scatter_on_vector(1, 0, VECTOR_ENTRIES)
+        nc.vector.tensor_tensor(new_last[:, 0:LATE], y_late[:], old_last[:, 0:LATE], MIN)
         scatter_on_vector(own, 0, T)
 
         pairs = pair_row[:].rearrange("p (a c e) -> p a c e", a=2, e=2)
@@ -155,22 +158,22 @@ def tile_picked_widxput_min_lo_kernel(tc, x_words, x_scales, mem, w1, slot, out_
             nc.gpsimd.tensor_scalar(pairs[:, 0, :, t], store[t][:], 1.0, -0.0, MULT, ADD)
 
         scatter_on_scalar(0, 0, HALF, picked[0][:, 0:HALF])
-        scatter_on_scalar(last, 0, EARLY, lent[:, 0:EARLY])
         scatter_on_scalar(0, HALF, T, picked[0][:, HALF:T])
         finish_early(0)
+        scatter_on_scalar(last, LATE, T, new_last[:, LATE:T])
         scatter_on_scalar(1, VECTOR_ENTRIES, T, picked[1][:, VECTOR_ENTRIES:T])
         finish_early(1)
-        scatter_on_scalar(last, EARLY, T, lent[:, EARLY:T])
-        for t in (last, own):
+        scatter_on_scalar(last, 0, LATE, new_last[:, 0:LATE])
+        for t in (own, last):
             nc.sync.dma_start(out_rows[:, t, :], store[t][:])
 
         grouped_row = keep.tile([P, U * PACK], BF16, name="grouped", align_bytes=64)
         grouped_words = grouped_row[:].bitcast(F32).rearrange("p (c a) -> p c a", a=2)
-        for t, lo, hi in ((last, 0, SCALAR_ROUNDS), (own, 0, PIECE), (own, PIECE, SCALAR_ROUNDS)):
+        for t, lo, hi in ((own, 0, SCALAR_ROUNDS), (last, 0, PIECE), (last, PIECE, SCALAR_ROUNDS)):
             nc.scalar.copy(pairs[:, 1, lo:hi, t % 2], store[t][:, lo:hi])
-        round_plane(last, SCALAR_ROUNDS, U)
-        round_plane(own, SCALAR_ROUNDS, U - PIECE)
-        round_plane(own, U - PIECE, U)
+        round_plane(own, SCALAR_ROUNDS, U)
+        round_plane(last, SCALAR_ROUNDS, U - PIECE)
+        round_plane(last, U - PIECE, U)
         for lo, hi in ((0, PIECE), (PIECE, SCALAR_WORDS)):
             nc.scalar.copy(grouped_words[:, lo:hi, :], pair_words[:, lo:hi, :])
         for lo, hi in ((SCALAR_WORDS, U - PIECE), (U - PIECE, U)):

@@ -24,7 +24,7 @@ W_VECTOR = 92
 FIRST = 128
 EARLY = 128
 LATE = T - EARLY
-SCALAR_GATHERS = 128
+SCALAR_GATHERS = 256
 PIECE = 256
 SCALAR_ROUNDS = 384
 SCALAR_WORDS = 512
@@ -96,15 +96,13 @@ def tile_picked_widxput_min_lo_kernel(tc, x_words, x_scales, mem, w1, slot, out_
 
         quantise_w(0, 1)
         y_first = [psum.tile([P, HALF], F32, name=f"y_first{h}") for h in range(2)]
-        y_early = psum.tile([P, EARLY], F32, name="y_early")
-        y_late = psum.tile([P, LATE], F32, name="y_late")
+        y_last = [psum.tile([P, HALF], F32, name=f"y_last{h}") for h in range(2)]
         y = {t: psum.tile([P, T], F32, name=f"y{t}") for t in (1, own)}
         one_pass(y_first[0][:], 0, 0, HALF)
         quantise_w(1, PACK)
         one_pass(y_first[1][:], 0, HALF, T)
-        one_pass(y_early[:], last, LATE, T)
-        for lo, hi in ((0, HALF), (HALF, LATE)):
-            one_pass(y_late[:, lo:hi], last, lo, hi)
+        one_pass(y_last[1][:], last, HALF, T)
+        one_pass(y_last[0][:], last, 0, HALF)
         for t in (1, own):
             one_pass(y[t][:], t, 0, T)
 
@@ -128,15 +126,15 @@ def tile_picked_widxput_min_lo_kernel(tc, x_words, x_scales, mem, w1, slot, out_
             nc.vector.tensor_copy(store[t][:].indirect(entries(lo, hi)), picked[t][:, lo:hi])
 
         halves = ((0, HALF), (HALF, T))
-        for lo, hi in ((FIRST, HALF), (HALF + FIRST, T)):
-            nc.scalar.activation(picked[0][:, lo:hi], store[0][:].indirect(entries(lo, hi)), COPY)
-        for lo in (0, HALF):
-            gather(picked[0][:, lo : lo + FIRST], 0, lo, lo + FIRST)
-        smaller(0, 0, HALF, y_first[0][:], picked[0][:, 0:HALF])
+        nc.scalar.activation(picked[0][:, HALF:T], store[0][:].indirect(entries(HALF, T)), COPY)
+        for lo, hi in ((0, FIRST), (FIRST, HALF)):
+            gather(picked[0][:, lo:hi], 0, lo, hi)
+        for lo, hi in ((0, FIRST), (FIRST, HALF)):
+            smaller(0, lo, hi, y_first[0][:, lo:hi], picked[0][:, lo:hi])
         nc.scalar.activation(old_last[:, 0:SCALAR_GATHERS], store[last][:].indirect(entries(0, SCALAR_GATHERS)), COPY)
         gather(old_last[:, SCALAR_GATHERS:T], last, SCALAR_GATHERS, T)
         smaller(0, HALF, T, y_first[1][:], picked[0][:, HALF:T])
-        nc.vector.tensor_tensor(new_last[:, LATE:T], y_early[:], old_last[:, LATE:T], MIN)
+        nc.vector.tensor_tensor(new_last[:, HALF:T], y_last[1][:], old_last[:, HALF:T], MIN)
         for t in (1, own):
             for old, (lo, hi) in zip(old_halves, halves):
                 gather(old, t, lo, hi)
@@ -144,7 +142,7 @@ def tile_picked_widxput_min_lo_kernel(tc, x_words, x_scales, mem, w1, slot, out_
                 smaller(t, lo, hi, y[t][:, lo:hi], old)
             if t == 1:
                 scatter_on_vector(1, 0, VECTOR_ENTRIES)
-        nc.vector.tensor_tensor(new_last[:, 0:LATE], y_late[:], old_last[:, 0:LATE], MIN)
+        nc.vector.tensor_tensor(new_last[:, 0:HALF], y_last[0][:], old_last[:, 0:HALF], MIN)
         scatter_on_vector(own, 0, T)
 
         pairs = pair_row[:].rearrange("p (a c e) -> p a c e", a=2, e=2)
@@ -157,8 +155,8 @@ def tile_picked_widxput_min_lo_kernel(tc, x_words, x_scales, mem, w1, slot, out_
             nc.sync.dma_start(out_rows[:, t, :], store[t][:])
             nc.gpsimd.tensor_scalar(pairs[:, 0, :, t], store[t][:], 1.0, -0.0, MULT, ADD)
 
-        scatter_on_scalar(0, 0, HALF, picked[0][:, 0:HALF])
-        scatter_on_scalar(0, HALF, T, picked[0][:, HALF:T])
+        scatter_on_scalar(0, 0, FIRST, picked[0][:, 0:FIRST])
+        scatter_on_scalar(0, FIRST, T, picked[0][:, FIRST:T])
         finish_early(0)
         scatter_on_scalar(last, LATE, T, new_last[:, LATE:T])
         scatter_on_scalar(1, VECTOR_ENTRIES, T, picked[1][:, VECTOR_ENTRIES:T])

@@ -26,9 +26,10 @@ EARLY = 128
 LATE = T - EARLY
 SCALAR_GATHERS = 256
 PIECE = 256
-SCALAR_ROUNDS = 384
-SCALAR_WORDS = 512
-STORED_PIECES = ((512, (768, 1024)), (0, (256,)), (256, (512,)))
+SCALAR_ROUNDS = 448
+SCALAR_WORDS = 384
+FIRST_STORED = 640
+STORED_PIECES = ((FIRST_STORED, (U,)), (PIECE, (FIRST_STORED,)), (0, (PIECE,)))
 VECTOR_ENTRIES = 128
 
 
@@ -167,14 +168,15 @@ def tile_picked_widxput_min_lo_kernel(tc, x_words, x_scales, mem, w1, slot, out_
 
         grouped_row = keep.tile([P, U * PACK], BF16, name="grouped", align_bytes=64)
         grouped_words = grouped_row[:].bitcast(F32).rearrange("p (c a) -> p c a", a=2)
-        for t, lo, hi in ((own, 0, SCALAR_ROUNDS), (last, 0, PIECE), (last, PIECE, SCALAR_ROUNDS)):
-            nc.scalar.copy(pairs[:, 1, lo:hi, t % 2], store[t][:, lo:hi])
+        for lo, hi in ((PIECE, SCALAR_ROUNDS), (0, PIECE)):
+            for t in (own, last):
+                nc.scalar.copy(pairs[:, 1, lo:hi, t % 2], store[t][:, lo:hi])
         round_plane(own, SCALAR_ROUNDS, U)
-        round_plane(last, SCALAR_ROUNDS, U - PIECE)
-        round_plane(last, U - PIECE, U)
-        for lo, hi in ((0, PIECE), (PIECE, SCALAR_WORDS)):
+        round_plane(last, FIRST_STORED, U)
+        round_plane(last, SCALAR_ROUNDS, FIRST_STORED)
+        for lo, hi in ((PIECE, SCALAR_WORDS), (0, PIECE)):
             nc.scalar.copy(grouped_words[:, lo:hi, :], pair_words[:, lo:hi, :])
-        for lo, hi in ((SCALAR_WORDS, U - PIECE), (U - PIECE, U)):
+        for lo, hi in ((FIRST_STORED, U), (SCALAR_WORDS, FIRST_STORED)):
             nc.vector.tensor_copy(grouped_words[:, lo:hi, :], pair_words[:, lo:hi, :])
 
         words = out_1[0].rearrange("p c r -> p (c r)").bitcast(I32)

@@ -19,18 +19,20 @@ COPY = mybir.ActivationFunctionType.Copy
 
 P = 128
 PACK = 4
+QUADRANTS = 4
 HALF = T // 2
+VECTOR_WINDOW = 2
+LAST_WINDOW = 3
+
 W_VECTOR = 92
-FIRST = 128
-EARLY = 128
-LATE = T - EARLY
-SCALAR_GATHERS = 256
-PIECE = 256
+FIRST = 160
+SCALAR_GATHERS = 192
+LATE = 384
+VECTOR_ENTRIES = 128
 SCALAR_ROUNDS = 448
 SCALAR_WORDS = 384
+LAST_STORED = 256
 FIRST_STORED = 640
-STORED_PIECES = ((FIRST_STORED, (U,)), (PIECE, (FIRST_STORED,)), (0, (PIECE,)))
-VECTOR_ENTRIES = 128
 
 
 def tile_picked_widxput_min_lo_kernel(tc, x_words, x_scales, mem, w1, slot, out_0, out_1, out_2):
@@ -41,7 +43,7 @@ def tile_picked_widxput_min_lo_kernel(tc, x_words, x_scales, mem, w1, slot, out_
 
         x_scale = keep.tile([P, T], U8, name="x_scale", align_bytes=64)
         x_scale_rows = x_scales[0].bitcast(I32)
-        for q in range(4):
+        for q in range(QUADRANTS):
             nc.scalar.dma_start(x_scale[32 * q : 32 * q + 4, :].bitcast(I32), x_scale_rows[4 * q : 4 * q + 4, :])
 
         w_rows = w1.rearrange("(p j) c -> p j c", j=PACK)
@@ -53,13 +55,13 @@ def tile_picked_widxput_min_lo_kernel(tc, x_words, x_scales, mem, w1, slot, out_
         offsets = keep.tile([P, T // 16], U16, name="offsets")
         x_codes = keep.tile([P, T], U32, name="x_codes", align_bytes=64)
         nc.sync.dma_start(offsets[:], slot)
-        nc.sync.dma_start(w_raw[0][:], w_rows[:, 0:2, :])
-        nc.sync.dma_start(w_raw[1][:], w_rows[:, 2:4, :])
+        for a in range(2):
+            nc.sync.dma_start(w_raw[a][:], w_rows[:, 2 * a : 2 * a + 2, :])
         nc.sync.dma_start(x_codes[:, 0:HALF].bitcast(I32), x_rows[:, 0:HALF])
-        nc.sync.dma_start(store[0][:], mem_rows[:, 0, :])
-        nc.sync.dma_start(store[3][:], mem_rows[:, 3, :])
+        for t in (0, LAST_WINDOW):
+            nc.sync.dma_start(store[t][:], mem_rows[:, t, :])
         nc.sync.dma_start(x_codes[:, HALF:T].bitcast(I32), x_rows[:, HALF:T])
-        for t in (1, 2):
+        for t in (1, VECTOR_WINDOW):
             nc.sync.dma_start(store[t][:], mem_rows[:, t, :])
 
         w_grouped = keep.tile([P, PACK * P * PACK], BF16, name="w_grouped", align_bytes=64)
@@ -71,11 +73,11 @@ def tile_picked_widxput_min_lo_kernel(tc, x_words, x_scales, mem, w1, slot, out_
         w_codes = keep.tile([P, N], U32, name="w_codes", align_bytes=64)
         w_scale = keep.tile([P, N], U8, name="w_scale", align_bytes=64)
 
-        def quantise_w(first, last):
+        def quantise_w(t_from, t_to):
             nc.vector.quantize_mx(
-                out=w_codes[:, first * P : last * P].bitcast(FP8X4),
-                scales=w_scale[:, first * P : last * P],
-                in_=w_grouped[:, first * P * PACK : last * P * PACK],
+                out=w_codes[:, t_from * P : t_to * P].bitcast(FP8X4),
+                scales=w_scale[:, t_from * P : t_to * P],
+                in_=w_grouped[:, t_from * P * PACK : t_to * P * PACK],
             )
 
         def one_pass(bank, t, lo, hi):
@@ -92,105 +94,112 @@ def tile_picked_widxput_min_lo_kernel(tc, x_words, x_scales, mem, w1, slot, out_
         def entries(lo, hi):
             return offsets[:, lo // 16 : hi // 16]
 
-        last = PACK - 1
-        own = PACK - 2
-
         quantise_w(0, 1)
         y_first = [psum.tile([P, HALF], F32, name=f"y_first{h}") for h in range(2)]
         y_last = [psum.tile([P, HALF], F32, name=f"y_last{h}") for h in range(2)]
-        y = {t: psum.tile([P, T], F32, name=f"y{t}") for t in (1, own)}
+        y = {t: psum.tile([P, T], F32, name=f"y{t}") for t in (1, VECTOR_WINDOW)}
         one_pass(y_first[0][:], 0, 0, HALF)
         quantise_w(1, PACK)
         one_pass(y_first[1][:], 0, HALF, T)
-        one_pass(y_last[1][:], last, HALF, T)
-        one_pass(y_last[0][:], last, 0, HALF)
-        for t in (1, own):
+        one_pass(y_last[1][:], LAST_WINDOW, HALF, T)
+        one_pass(y_last[0][:], LAST_WINDOW, 0, HALF)
+        for t in (1, VECTOR_WINDOW):
             one_pass(y[t][:], t, 0, T)
 
-        picked = {t: keep.tile([P, T], F32, name=f"picked{t}") for t in (0, 1, own)}
+        picked = {t: keep.tile([P, T], F32, name=f"picked{t}") for t in (0, 1, VECTOR_WINDOW)}
         old_last = keep.tile([P, T], F32, name="old_last")
         pair_row = keep.tile([P, U * PACK], BF16, name="pairs", align_bytes=64)
         new_last = keep.tile([P, T], F32, name="new_last")
         old_second = keep.tile([P, HALF], F32, name="old_second")
         old_halves = (new_last[:, 0:HALF], old_second[:])
 
-        def gather(out, t, lo, hi):
+        def gather_on_vector(out, t, lo, hi):
             nc.vector.tensor_copy(out, store[t][:].indirect(entries(lo, hi)))
 
-        def smaller(t, lo, hi, sums, old):
-            nc.vector.tensor_tensor(picked[t][:, lo:hi], sums, old, MIN)
+        def gather_on_scalar(out, t, lo, hi):
+            nc.scalar.activation(out, store[t][:].indirect(entries(lo, hi)), COPY)
 
-        def scatter_on_scalar(t, lo, hi, values):
-            nc.scalar.activation(store[t][:].indirect(entries(lo, hi)), values, COPY)
+        def smaller(out, sums, old):
+            nc.vector.tensor_tensor(out, sums, old, MIN)
 
         def scatter_on_vector(t, lo, hi):
             nc.vector.tensor_copy(store[t][:].indirect(entries(lo, hi)), picked[t][:, lo:hi])
 
+        def scatter_on_scalar(t, lo, hi, values):
+            nc.scalar.activation(store[t][:].indirect(entries(lo, hi)), values[:, lo:hi], COPY)
+
         halves = ((0, HALF), (HALF, T))
-        nc.scalar.activation(picked[0][:, HALF:T], store[0][:].indirect(entries(HALF, T)), COPY)
-        for lo, hi in ((0, FIRST), (FIRST, HALF)):
-            gather(picked[0][:, lo:hi], 0, lo, hi)
-        for lo, hi in ((0, FIRST), (FIRST, HALF)):
-            smaller(0, lo, hi, y_first[0][:, lo:hi], picked[0][:, lo:hi])
-        nc.scalar.activation(old_last[:, 0:SCALAR_GATHERS], store[last][:].indirect(entries(0, SCALAR_GATHERS)), COPY)
-        gather(old_last[:, SCALAR_GATHERS:T], last, SCALAR_GATHERS, T)
-        smaller(0, HALF, T, y_first[1][:], picked[0][:, HALF:T])
-        nc.vector.tensor_tensor(new_last[:, HALF:T], y_last[1][:], old_last[:, HALF:T], MIN)
-        for t in (1, own):
+        first_pieces = ((0, FIRST), (FIRST, HALF))
+        gather_on_scalar(picked[0][:, HALF:T], 0, HALF, T)
+        for lo, hi in first_pieces:
+            gather_on_vector(picked[0][:, lo:hi], 0, lo, hi)
+        for lo, hi in first_pieces:
+            smaller(picked[0][:, lo:hi], y_first[0][:, lo:hi], picked[0][:, lo:hi])
+        gather_on_scalar(old_last[:, 0:SCALAR_GATHERS], LAST_WINDOW, 0, SCALAR_GATHERS)
+        gather_on_vector(old_last[:, SCALAR_GATHERS:T], LAST_WINDOW, SCALAR_GATHERS, T)
+        smaller(picked[0][:, HALF:T], y_first[1][:], picked[0][:, HALF:T])
+        smaller(new_last[:, HALF:T], y_last[1][:], old_last[:, HALF:T])
+
+        def new_values(t):
             for old, (lo, hi) in zip(old_halves, halves):
-                gather(old, t, lo, hi)
+                gather_on_vector(old, t, lo, hi)
             for old, (lo, hi) in zip(old_halves, halves):
-                smaller(t, lo, hi, y[t][:, lo:hi], old)
-            if t == 1:
-                scatter_on_vector(1, 0, VECTOR_ENTRIES)
-        nc.vector.tensor_tensor(new_last[:, 0:HALF], y_last[0][:], old_last[:, 0:HALF], MIN)
-        scatter_on_vector(own, 0, T)
+                smaller(picked[t][:, lo:hi], y[t][:, lo:hi], old)
+
+        new_values(1)
+        scatter_on_vector(1, 0, VECTOR_ENTRIES)
+        new_values(VECTOR_WINDOW)
+        smaller(new_last[:, 0:HALF], y_last[0][:], old_last[:, 0:HALF])
+        scatter_on_vector(VECTOR_WINDOW, 0, T)
 
         pairs = pair_row[:].rearrange("p (a c e) -> p a c e", a=2, e=2)
         pair_words = pair_row[:].bitcast(F32).rearrange("p (a c) -> p c a", a=2)
 
-        def round_plane(t, lo, hi):
+        def round_on_vector(t, lo, hi):
             nc.vector.tensor_copy(pairs[:, t // 2, lo:hi, t % 2], store[t][:, lo:hi])
+
+        def round_on_scalar(t, lo, hi):
+            nc.scalar.copy(pairs[:, t // 2, lo:hi, t % 2], store[t][:, lo:hi])
 
         def finish_early(t):
             nc.sync.dma_start(out_rows[:, t, :], store[t][:])
             nc.gpsimd.tensor_scalar(pairs[:, 0, :, t], store[t][:], 1.0, -0.0, MULT, ADD)
 
-        scatter_on_scalar(0, 0, FIRST, picked[0][:, 0:FIRST])
-        scatter_on_scalar(0, FIRST, T, picked[0][:, FIRST:T])
+        scatter_on_scalar(0, 0, FIRST, picked[0])
+        scatter_on_scalar(0, FIRST, T, picked[0])
         finish_early(0)
-        scatter_on_scalar(last, LATE, T, new_last[:, LATE:T])
-        scatter_on_scalar(1, VECTOR_ENTRIES, T, picked[1][:, VECTOR_ENTRIES:T])
+        scatter_on_scalar(LAST_WINDOW, LATE, T, new_last)
+        scatter_on_scalar(1, VECTOR_ENTRIES, T, picked[1])
         finish_early(1)
-        scatter_on_scalar(last, 0, LATE, new_last[:, 0:LATE])
-        for t in (own, last):
+        scatter_on_scalar(LAST_WINDOW, 0, LATE, new_last)
+
+        for t in (VECTOR_WINDOW, LAST_WINDOW):
             nc.sync.dma_start(out_rows[:, t, :], store[t][:])
 
         grouped_row = keep.tile([P, U * PACK], BF16, name="grouped", align_bytes=64)
         grouped_words = grouped_row[:].bitcast(F32).rearrange("p (c a) -> p c a", a=2)
-        for lo, hi in ((PIECE, SCALAR_ROUNDS), (0, PIECE)):
-            for t in (own, last):
-                nc.scalar.copy(pairs[:, 1, lo:hi, t % 2], store[t][:, lo:hi])
-        round_plane(own, SCALAR_ROUNDS, U)
-        round_plane(last, FIRST_STORED, U)
-        round_plane(last, SCALAR_ROUNDS, FIRST_STORED)
-        for lo, hi in ((PIECE, SCALAR_WORDS), (0, PIECE)):
+        for lo, hi in ((LAST_STORED, SCALAR_ROUNDS), (0, LAST_STORED)):
+            for t in (VECTOR_WINDOW, LAST_WINDOW):
+                round_on_scalar(t, lo, hi)
+        round_on_vector(VECTOR_WINDOW, SCALAR_ROUNDS, U)
+        round_on_vector(LAST_WINDOW, FIRST_STORED, U)
+        round_on_vector(LAST_WINDOW, SCALAR_ROUNDS, FIRST_STORED)
+        for lo, hi in ((LAST_STORED, SCALAR_WORDS), (0, LAST_STORED)):
             nc.scalar.copy(grouped_words[:, lo:hi, :], pair_words[:, lo:hi, :])
         for lo, hi in ((FIRST_STORED, U), (SCALAR_WORDS, FIRST_STORED)):
             nc.vector.tensor_copy(grouped_words[:, lo:hi, :], pair_words[:, lo:hi, :])
 
         words = out_1[0].rearrange("p c r -> p (c r)").bitcast(I32)
         o_scale = keep.tile([P, U], U8, name="o_scale", align_bytes=64)
-        for first, cuts in STORED_PIECES:
-            o_codes = keep.tile([P, cuts[-1] - first], U32, name=f"o_codes{first}", align_bytes=64)
-            for lo, hi in zip((first,) + cuts, cuts):
-                nc.vector.quantize_mx(
-                    out=o_codes[:, lo - first : hi - first].bitcast(FP8X4),
-                    scales=o_scale[:, lo:hi],
-                    in_=grouped_row[:, PACK * lo : PACK * hi],
-                )
-            nc.sync.dma_start(words[:, first : cuts[-1]], o_codes[:].bitcast(I32))
+        for lo, hi in ((FIRST_STORED, U), (LAST_STORED, FIRST_STORED), (0, LAST_STORED)):
+            o_codes = keep.tile([P, hi - lo], U32, name=f"o_codes{lo}", align_bytes=64)
+            nc.vector.quantize_mx(
+                out=o_codes[:].bitcast(FP8X4),
+                scales=o_scale[:, lo:hi],
+                in_=grouped_row[:, PACK * lo : PACK * hi],
+            )
+            nc.sync.dma_start(words[:, lo:hi], o_codes[:].bitcast(I32))
         scale_rows = out_2[0].bitcast(I32)
-        for q in range(4):
-            queue = nc.scalar if q < 2 else nc.sync
+        for q in range(QUADRANTS):
+            queue = nc.scalar if q < QUADRANTS // 2 else nc.sync
             queue.dma_start(scale_rows[4 * q : 4 * q + 4, :], o_scale[32 * q : 32 * q + 4, :].bitcast(I32))

from contextlib import ExitStack

import concourse.mybir as mybir

K, T, N, U = 512, 512, 512, 1024
FLOPS = 2 * K * T * N

F32 = mybir.dt.float32
BF16 = mybir.dt.bfloat16
I32 = mybir.dt.int32
U32 = mybir.dt.uint32
U16 = mybir.dt.uint16
U8 = mybir.dt.uint8
FP8X4 = mybir.dt.float8_e4m3fn_x4
MIN = mybir.AluOpType.min
MULT = mybir.AluOpType.mult
ADD = mybir.AluOpType.add
COPY = mybir.ActivationFunctionType.Copy

P = 128
PACK = 4
QUADRANTS = 4
HALF = T // 2
VECTOR_WINDOW = 2
LAST_WINDOW = 3

W_VECTOR = 92
FIRST = 160
SCALAR_GATHERS = 192
LATE = 384
VECTOR_ENTRIES = 128
SCALAR_ROUNDS = 448
SCALAR_WORDS = 384
LAST_STORED = 256
FIRST_STORED = 640


def tile_picked_widxput_min_lo_kernel(tc, x_words, x_scales, mem, w1, slot, out_0, out_1, out_2):
    nc = tc.nc
    with ExitStack() as ctx:
        keep = ctx.enter_context(tc.tile_pool(name="keep", bufs=1))
        psum = ctx.enter_context(tc.psum_pool(name="psum", bufs=1))

        x_scale = keep.tile([P, T], U8, name="x_scale", align_bytes=64)
        x_scale_rows = x_scales[0].bitcast(I32)
        for q in range(QUADRANTS):
            nc.scalar.dma_start(x_scale[32 * q : 32 * q + 4, :].bitcast(I32), x_scale_rows[4 * q : 4 * q + 4, :])

        w_rows = w1.rearrange("(p j) c -> p j c", j=PACK)
        mem_rows = mem.rearrange("(p t) u -> p t u", t=PACK)
        out_rows = out_0.rearrange("(p t) u -> p t u", t=PACK)
        x_rows = x_words[0].rearrange("p c r -> p (c r)").bitcast(I32)
        w_raw = [keep.tile([P, PACK // 2, N], F32, name=f"w_raw{a}") for a in range(2)]
        store = [keep.tile([P, U], F32, name=f"store{t}") for t in range(PACK)]
        offsets = keep.tile([P, T // 16], U16, name="offsets")
        x_codes = keep.tile([P, T], U32, name="x_codes", align_bytes=64)
        nc.sync.dma_start(offsets[:], slot)
        for a in range(2):
            nc.sync.dma_start(w_raw[a][:], w_rows[:, 2 * a : 2 * a + 2, :])
        nc.sync.dma_start(x_codes[:, 0:HALF].bitcast(I32), x_rows[:, 0:HALF])
        for t in (0, LAST_WINDOW):
            nc.sync.dma_start(store[t][:], mem_rows[:, t, :])
        nc.sync.dma_start(x_codes[:, HALF:T].bitcast(I32), x_rows[:, HALF:T])
        for t in (1, VECTOR_WINDOW):
            nc.sync.dma_start(store[t][:], mem_rows[:, t, :])

        w_grouped = keep.tile([P, PACK * P * PACK], BF16, name="w_grouped", align_bytes=64)
        w_dealt = w_grouped[:].rearrange("p (t m j) -> p m j t", t=PACK, j=PACK)
        for a in range(2):
            source = w_raw[a][:].rearrange("p j (m t) -> p m j t", t=PACK)
            nc.vector.tensor_copy(w_dealt[:, 0:W_VECTOR, 2 * a : 2 * a + 2, :], source[:, 0:W_VECTOR, :, :])
            nc.scalar.activation(w_dealt[:, W_VECTOR:, 2 * a : 2 * a + 2, :], source[:, W_VECTOR:, :, :], COPY)
        w_codes = keep.tile([P, N], U32, name="w_codes", align_bytes=64)
        w_scale = keep.tile([P, N], U8, name="w_scale", align_bytes=64)

        def quantise_w(t_from, t_to):
            nc.vector.quantize_mx(
                out=w_codes[:, t_from * P : t_to * P].bitcast(FP8X4),
                scales=w_scale[:, t_from * P : t_to * P],
                in_=w_grouped[:, t_from * P * PACK : t_to * P * PACK],
            )

        def one_pass(bank, t, lo, hi):
            nc.tensor.matmul_mx(
                out=bank,
                lhsT=w_codes[:, t * P : (t + 1) * P].bitcast(FP8X4),
                lhsT_scale=w_scale[:, t * P : (t + 1) * P],
                rhs=x_codes[:, lo:hi].bitcast(FP8X4),
                rhs_scale=x_scale[:, lo:hi],
                start=True,
                stop=True,
            )

        def entries(lo, hi):
            return offsets[:, lo // 16 : hi // 16]

        quantise_w(0, 1)
        y_first = [psum.tile([P, HALF], F32, name=f"y_first{h}") for h in range(2)]
        y_last = [psum.tile([P, HALF], F32, name=f"y_last{h}") for h in range(2)]
        y = {t: psum.tile([P, T], F32, name=f"y{t}") for t in (1, VECTOR_WINDOW)}
        one_pass(y_first[0][:], 0, 0, HALF)
        quantise_w(1, PACK)
        one_pass(y_first[1][:], 0, HALF, T)
        one_pass(y_last[1][:], LAST_WINDOW, HALF, T)
        one_pass(y_last[0][:], LAST_WINDOW, 0, HALF)
        for t in (1, VECTOR_WINDOW):
            one_pass(y[t][:], t, 0, T)

        picked = {t: keep.tile([P, T], F32, name=f"picked{t}") for t in (0, 1, VECTOR_WINDOW)}
        old_last = keep.tile([P, T], F32, name="old_last")
        pair_row = keep.tile([P, U * PACK], BF16, name="pairs", align_bytes=64)
        new_last = keep.tile([P, T], F32, name="new_last")
        old_second = keep.tile([P, HALF], F32, name="old_second")
        old_halves = (new_last[:, 0:HALF], old_second[:])

        def gather_on_vector(out, t, lo, hi):
            nc.vector.tensor_copy(out, store[t][:].indirect(entries(lo, hi)))

        def gather_on_scalar(out, t, lo, hi):
            nc.scalar.activation(out, store[t][:].indirect(entries(lo, hi)), COPY)

        def smaller(out, sums, old):
            nc.vector.tensor_tensor(out, sums, old, MIN)

        def scatter_on_vector(t, lo, hi):
            nc.vector.tensor_copy(store[t][:].indirect(entries(lo, hi)), picked[t][:, lo:hi])

        def scatter_on_scalar(t, lo, hi, values):
            nc.scalar.activation(store[t][:].indirect(entries(lo, hi)), values[:, lo:hi], COPY)

        halves = ((0, HALF), (HALF, T))
        first_pieces = ((0, FIRST), (FIRST, HALF))
        gather_on_scalar(picked[0][:, HALF:T], 0, HALF, T)
        for lo, hi in first_pieces:
            gather_on_vector(picked[0][:, lo:hi], 0, lo, hi)
        for lo, hi in first_pieces:
            smaller(picked[0][:, lo:hi], y_first[0][:, lo:hi], picked[0][:, lo:hi])
        gather_on_scalar(old_last[:, 0:SCALAR_GATHERS], LAST_WINDOW, 0, SCALAR_GATHERS)
        gather_on_vector(old_last[:, SCALAR_GATHERS:T], LAST_WINDOW, SCALAR_GATHERS, T)
        smaller(picked[0][:, HALF:T], y_first[1][:], picked[0][:, HALF:T])
        smaller(new_last[:, HALF:T], y_last[1][:], old_last[:, HALF:T])

        def new_values(t):
            for old, (lo, hi) in zip(old_halves, halves):
                gather_on_vector(old, t, lo, hi)
            for old, (lo, hi) in zip(old_halves, halves):
                smaller(picked[t][:, lo:hi], y[t][:, lo:hi], old)

        new_values(1)
        scatter_on_vector(1, 0, VECTOR_ENTRIES)
        new_values(VECTOR_WINDOW)
        smaller(new_last[:, 0:HALF], y_last[0][:], old_last[:, 0:HALF])
        scatter_on_vector(VECTOR_WINDOW, 0, T)

        pairs = pair_row[:].rearrange("p (a c e) -> p a c e", a=2, e=2)
        pair_words = pair_row[:].bitcast(F32).rearrange("p (a c) -> p c a", a=2)

        def round_on_vector(t, lo, hi):
            nc.vector.tensor_copy(pairs[:, t // 2, lo:hi, t % 2], store[t][:, lo:hi])

        def round_on_scalar(t, lo, hi):
            nc.scalar.copy(pairs[:, t // 2, lo:hi, t % 2], store[t][:, lo:hi])

        def finish_early(t):
            nc.sync.dma_start(out_rows[:, t, :], store[t][:])
            nc.gpsimd.tensor_scalar(pairs[:, 0, :, t], store[t][:], 1.0, -0.0, MULT, ADD)

        scatter_on_scalar(0, 0, FIRST, picked[0])
        scatter_on_scalar(0, FIRST, T, picked[0])
        finish_early(0)
        scatter_on_scalar(LAST_WINDOW, LATE, T, new_last)
        scatter_on_scalar(1, VECTOR_ENTRIES, T, picked[1])
        finish_early(1)
        scatter_on_scalar(LAST_WINDOW, 0, LATE, new_last)

        for t in (VECTOR_WINDOW, LAST_WINDOW):
            nc.sync.dma_start(out_rows[:, t, :], store[t][:])

        grouped_row = keep.tile([P, U * PACK], BF16, name="grouped", align_bytes=64)
        grouped_words = grouped_row[:].bitcast(F32).rearrange("p (c a) -> p c a", a=2)
        for lo, hi in ((LAST_STORED, SCALAR_ROUNDS), (0, LAST_STORED)):
            for t in (VECTOR_WINDOW, LAST_WINDOW):
                round_on_scalar(t, lo, hi)
        round_on_vector(VECTOR_WINDOW, SCALAR_ROUNDS, U)
        round_on_vector(LAST_WINDOW, FIRST_STORED, U)
        round_on_vector(LAST_WINDOW, SCALAR_ROUNDS, FIRST_STORED)
        for lo, hi in ((LAST_STORED, SCALAR_WORDS), (0, LAST_STORED)):
            nc.scalar.copy(grouped_words[:, lo:hi, :], pair_words[:, lo:hi, :])
        for lo, hi in ((FIRST_STORED, U), (SCALAR_WORDS, FIRST_STORED)):
            nc.vector.tensor_copy(grouped_words[:, lo:hi, :], pair_words[:, lo:hi, :])

        words = out_1[0].rearrange("p c r -> p (c r)").bitcast(I32)
        o_scale = keep.tile([P, U], U8, name="o_scale", align_bytes=64)
        for lo, hi in ((FIRST_STORED, U), (LAST_STORED, FIRST_STORED), (0, LAST_STORED)):
            o_codes = keep.tile([P, hi - lo], U32, name=f"o_codes{lo}", align_bytes=64)
            nc.vector.quantize_mx(
                out=o_codes[:].bitcast(FP8X4),
                scales=o_scale[:, lo:hi],
                in_=grouped_row[:, PACK * lo : PACK * hi],
            )
            nc.sync.dma_start(words[:, lo:hi], o_codes[:].bitcast(I32))
        scale_rows = out_2[0].bitcast(I32)
        for q in range(QUADRANTS):
            queue = nc.scalar if q < QUADRANTS // 2 else nc.sync
            queue.dma_start(scale_rows[4 * q : 4 * q + 4, :], o_scale[32 * q : 32 * q + 4, :].bitcast(I32))
